import numpy as np
import ml_dtypes


def mxq(x, axis, fmt="e4m3"):
    dtype, down = {"e4m3": (ml_dtypes.float8_e4m3fn, 7), "e5m2": (ml_dtypes.float8_e5m2, 14)}[fmt]
    v = np.moveaxis(np.asarray(x, np.float32).astype(ml_dtypes.bfloat16).astype(np.float64), axis, -1)
    blocks = v.reshape(v.shape[:-1] + (-1, 32))
    amax = np.abs(blocks).max(-1, keepdims=True)
    byte = np.maximum(np.where(amax > 0, np.frexp(amax)[1] - 1 + 127, 0) - down, 1)
    scale = np.exp2(byte - 127.0)
    codes = (blocks / scale).astype(np.float32).astype(dtype).astype(np.float64)
    return np.moveaxis((codes * scale).reshape(v.shape), -1, axis)


WIDE = False


def mx_kscale(k):
    if not WIDE:
        return np.ones(k)
    levels = np.array([10, -10, 5, -5, 0])
    if k % 512:
        return np.exp2(np.random.permutation(np.resize(levels, k // 32))).repeat(32)
    a = np.empty((k // 512, 16))
    for p in range(k // 512):
        a[p, :8] = np.random.permutation(np.resize(levels, 8))
        for g in range(8):
            far = levels[np.abs(levels - a[p, g]) >= 10]
            a[p, g + 8] = far[np.random.randint(len(far))]
    return np.exp2(a.ravel()).repeat(32)


BF16 = ml_dtypes.bfloat16


def bf(x):
    return np.asarray(x, np.float32).astype(BF16)


def f64(x):
    return np.asarray(x).astype(np.float64)


E2M1 = np.array([0.0, 0.5, 1.0, 1.5, 2.0, 3.0, 4.0, 6.0, -0.0, -0.5, -1.0, -1.5, -2.0, -3.0, -4.0, -6.0])


def pack_weight(w, fmt):
    k, n = w.shape
    w = f64(bf(w)).reshape(k // 32, 32, n)
    amax = np.abs(w).max(1)
    if fmt == "e4m3":
        byte = np.frexp(amax)[1] - 1 + 127 - 7
    else:
        mant, ex = np.frexp(amax / 6.0)
        byte = np.where(mant > 0.5, ex, ex - 1) + 127
    byte = np.clip(np.where(amax > 0, byte, 1), 1, 254)
    scaled = (w * np.exp2(127.0 - byte)[:, None, :]).reshape(k, n).astype(np.float32)
    by_word = np.ascontiguousarray(scaled.reshape(k // 512, 128, 4, n).transpose(0, 1, 3, 2))
    if fmt == "e4m3":
        words = by_word.astype(ml_dtypes.float8_e4m3fn).view(np.uint8)
    else:
        c = by_word.astype(ml_dtypes.float4_e2m1fn).view(np.uint8) & 0xF
        words = c[..., 0::2] | (c[..., 1::2] << 4)
    return np.ascontiguousarray(words), np.ascontiguousarray(byte.astype(np.uint8).reshape(k // 512, 16, n))


def unpack_weight(words, scales, fmt):
    g, p, n, _ = words.shape
    if fmt == "e4m3":
        vals = np.ascontiguousarray(words).view(ml_dtypes.float8_e4m3fn).astype(np.float64)
    else:
        nib = np.empty((g, p, n, 4), np.uint8)
        nib[..., 0::2] = words & 0xF
        nib[..., 1::2] = words >> 4
        vals = E2M1[nib]
    vals = vals * np.repeat(np.exp2(scales.astype(np.float64) - 127.0), 8, axis=1)[..., None]
    return vals.transpose(0, 1, 3, 2).reshape(g * 512, n)
def pack4(w):
    words, scales = pack_weight(w, "e2m1")
    return words.reshape(words.shape[0], 128, -1), scales


def unpack4(words, scales):
    return unpack_weight(words.reshape(words.shape[0], 128, -1, 2), scales, "e2m1")


def planes(Y):
    n, m = Y.shape
    b = f64(bf(Y)).reshape(n // 32, 32, m)
    amax = np.abs(b).max(1)
    byte = np.clip(np.where(amax > 0, np.frexp(amax)[1] - 1 + 127 - 7, 1), 1, 254)
    codes = (b * np.exp2(127.0 - byte)[:, None, :]).reshape(n, m).astype(np.float32).astype(ml_dtypes.float8_e4m3fn).view(np.uint8)
    words = codes.reshape(n // 512, 128, 4, m).transpose(0, 1, 3, 2)
    return np.ascontiguousarray(words), np.ascontiguousarray(byte.astype(np.uint8).reshape(n // 512, 16, m))


M, D, F, N = 1024, 2048, 1536, 1024


def setup_inputs():
    s = mx_kscale(D)
    t = mx_kscale(F)
    x = bf(np.random.randn(M, D) * s)
    w1_words, w1_scales = pack4(np.random.randn(D, F) / np.sqrt(D) / s[:, None])
    w2_words, w2_scales = pack4(1.5 * np.random.randn(F, N) / np.sqrt(F) / t[:, None])
    gain = bf((1 + 0.2 * np.random.randn(F)) * t)
    bias = bf(0.3 * np.random.randn(N))
    reward_weight = bf(np.sign(np.random.randn(N)) * np.exp(0.8 * np.random.randn(N)))
    return {"x": x, "w1_words": w1_words, "w1_scales": w1_scales, "gain": gain,
            "w2_words": w2_words, "w2_scales": w2_scales, "bias": bias,
            "reward_weight": reward_weight}


def reference(x, w1_words, w1_scales, gain, w2_words, w2_scales, bias, reward_weight):
    w1 = unpack4(w1_words, w1_scales)
    w2 = unpack4(w2_words, w2_scales)
    a = mxq(f64(x), 1, "e4m3") @ w1
    h = np.tanh(a) * f64(gain)
    z = mxq(h, 1, "e4m3") @ w2
    u = np.tanh(z + f64(bias))
    y = u * f64(reward_weight)
    words, scales = planes(y.T)
    return y, words, scales

@@ -1,0 +1,433 @@
+from contextlib import ExitStack
+
+import concourse.mybir as mybir
+from concourse.masks import make_identity
+
+M, D, F, N = 1024, 2048, 1536, 1024
+FLOPS = 2 * M * (D * F + F * N)
+
+F32 = mybir.dt.float32
+BF16 = mybir.dt.bfloat16
+I32 = mybir.dt.int32
+U32 = mybir.dt.uint32
+U8 = mybir.dt.uint8
+FP8X4 = mybir.dt.float8_e4m3fn_x4
+FP4X4 = mybir.dt.float4_e2m1fn_x4
+TANH = mybir.ActivationFunctionType.Tanh
+ADD = mybir.AluOpType.add
+MULT = mybir.AluOpType.mult
+
+P = 128
+GROUP = 512
+TILES = M // P
+GD, GF, GN = D // GROUP, F // GROUP, N // GROUP
+
+
+def tile_reward_head_terms_h1_kernel(tc, x, w1_words, w1_scales, gain, w2_words, w2_scales, bias,
+                                                reward_weight, out_0, out_1, out_2):
+    nc = tc.nc
+    with ExitStack() as ctx:
+        keep = ctx.enter_context(tc.tile_pool(name="keep", bufs=1))
+        work = ctx.enter_context(tc.tile_pool(name="work", bufs=4))
+        turn = ctx.enter_context(tc.psum_pool(name="turn", bufs=1))
+        sums = ctx.enter_context(tc.psum_pool(name="sums", bufs=3))
+        ctx.enter_context(tc.manual_schedule())
+
+        ident = keep.tile([P, P], F32, name="ident", align_bytes=64)
+        make_identity(nc, ident[:])
+
+        x_sb = [keep.tile([P, D], BF16, name="x_sb%d" % i, align_bytes=64) for i in range(TILES)]
+        w1_sb = [keep.tile([P, GD, 2 * GROUP], U8, name="w1_sb%d" % c, align_bytes=64) for c in range(GF)]
+        s1_sb = [keep.tile([P, GD, GROUP], U8, name="s1_sb%d" % c, align_bytes=64) for c in range(GF)]
+        w2_sb = keep.tile([P, GF, 2 * N], U8, name="w2_sb", align_bytes=64)
+        s2_sb = keep.tile([P, GF, N], U8, name="s2_sb", align_bytes=64)
+        gain_col = keep.tile([P, GF, 4], BF16, name="gain_col", align_bytes=64)
+        bias_col = keep.tile([P, GN, 2, 2], BF16, name="bias_col", align_bytes=64)
+        rw_col = keep.tile([P, GN, 2, 2], BF16, name="rw_col", align_bytes=64)
+        gain_all = keep.tile([P, F], BF16, name="gain_all", align_bytes=64)
+        bias_all = keep.tile([P, N], BF16, name="bias_all", align_bytes=64)
+        rw_all = keep.tile([P, N], BF16, name="rw_all", align_bytes=64)
+        y_codes = keep.tile([P, GN, M], U32, name="y_codes", align_bytes=64)
+        y_scales = keep.tile([P, GN, M], U8, name="y_scales", align_bytes=64)
+        warm = keep.tile([P, 2], F32, name="warm", align_bytes=64)
+
+        for c in range(GF):
+            nc.vector.memset(s1_sb[c][:].rearrange("p g n -> p (g n)").bitcast(I32), 0)
+        nc.vector.memset(s2_sb[:].rearrange("p g n -> p (g n)").bitcast(I32), 0)
+        nc.gpsimd.memset(warm[:, 0:1], 0.0)
+
+        def load_x(i, k0, k1):
+            nc.sync.dma_start(out=x_sb[i][:, k0:k1], in_=x[i * P:(i + 1) * P, k0:k1])
+
+        def load_scales(plane, rows, n0, n1):
+            for q in range(4):
+                nc.sync.dma_start(
+                    out=plane[32 * q:32 * q + 4].bitcast(I32),
+                    in_=rows[:, 4 * q:4 * q + 4, n0:n1].rearrange("g r n -> r g n").bitcast(I32))
+
+        def load_w1(c, pieces):
+            load_scales(s1_sb[c], w1_scales, c * GROUP, (c + 1) * GROUP)
+            step = GD // pieces
+            for g in range(0, GD, step):
+                nc.sync.dma_start(
+                    out=w1_sb[c][:, g:g + step, :].bitcast(I32),
+                    in_=w1_words[g:g + step, :, 2 * c * GROUP:2 * (c + 1) * GROUP].rearrange("g p b -> p g b").bitcast(I32))
+
+        nc.scalar.dma_start(out=gain_col[:], in_=gain.rearrange("(c p t) -> p c t", p=P, t=4))
+        nc.scalar.activation(out=warm[:, 1:2], in_=warm[:, 0:1], func=TANH)
+        load_x(0, 0, D // 2)
+        load_x(0, D // 2, D)
+        load_w1(0, 2)
+        load_x(1, 0, D)
+        nc.sync.dma_start(out=bias_col[:].rearrange("p c u e -> p c (u e)"), in_=bias.rearrange("(c p t) -> p c t", p=P, t=4))
+        nc.sync.dma_start(out=rw_col[:].rearrange("p c u e -> p c (u e)"), in_=reward_weight.rearrange("(c p t) -> p c t", p=P, t=4))
+        load_w1(1, 1)
+        load_w1(2, 1)
+        load_x(2, 0, D)
+        load_scales(s2_sb, w2_scales, 0, N)
+        nc.sync.dma_start(out=w2_sb[:].bitcast(I32), in_=w2_words.rearrange("g p b -> p g b").bitcast(I32))
+        for i in range(3, TILES):
+            load_x(i, 0, D)
+
+        t = {}
+
+        def live(i):
+            return 0 <= i < TILES
+
+        def x_turn(i, tags=("x_bank0", "x_bank1")):
+            if not live(i):
+                return
+            words = x_sb[i][:].bitcast(F32)
+            groups = GD // len(tags)
+            for b, tag in enumerate(tags):
+                bank = turn.tile([P, groups, 2, P], F32, name="x_bank%d_%d" % (i, b), tag=tag)
+                t["x_bank", i, b] = bank
+                for g in range(groups):
+                    for u in range(2):
+                        w0 = 256 * (groups * b + g)
+                        nc.tensor.transpose(bank[:, g, u, :], words[:, w0 + u:w0 + 256:2], ident[:])
+            t["x_rows", i] = work.tile([P, GD, P, 4], BF16, name="x_rows%d" % i, tag="x_rows", align_bytes=64)
+            t["x_codes", i] = work.tile([P, GD * P], U32, name="x_codes%d" % i, tag="x_codes", align_bytes=64)
+            t["x_scales", i] = work.tile([P, GD * P], U8, name="x_scales%d" % i, tag="x_scales", align_bytes=64)
+
+        def interleave(rows, bank):
+            nc.scalar.copy(out=rows.bitcast(F32), in_=bank.rearrange("p g u r -> p g r u"))
+
+        def quantize(codes, scales, rows):
+            nc.vector.quantize_mx(out=codes.bitcast(FP8X4), scales=scales, in_=rows.rearrange("p g r t -> p (g r t)"))
+
+        def x_copy(i, b, groups=2):
+            if live(i):
+                interleave(t["x_rows", i][:, groups * b:groups * (b + 1)], t["x_bank", i, b][:])
+
+        def x_quant(i, g0, g1):
+            if live(i):
+                quantize(t["x_codes", i][:, g0 * P:g1 * P], t["x_scales", i][:, g0 * P:g1 * P], t["x_rows", i][:, g0:g1])
+
+        def mm1(i, c):
+            if not live(i):
+                return
+            acc = sums.tile([P, GROUP], F32, name="a%d_%d" % (i, c), tag="acc")
+            t["a", i, c] = acc
+            for g in range(GD):
+                nc.tensor.matmul_mx(
+                    out=acc[:],
+                    lhsT=t["x_codes", i][:, g * P:(g + 1) * P].bitcast(FP8X4),
+                    lhsT_scale=t["x_scales", i][:, g * P:(g + 1) * P],
+                    rhs=w1_sb[c][:, g, :].bitcast(FP4X4),
+                    rhs_scale=s1_sb[c][:, g, :],
+                    start=(g == 0), stop=(g == GD - 1))
+
+        def once(kind, i, c, shape, dtype):
+            if (kind, i, c) not in t:
+                t[kind, i, c] = work.tile(shape, dtype, name="%s%d_%d" % (kind, i, c), tag=kind, align_bytes=64)
+            return t[kind, i, c]
+
+        def by_half(ap, c=0):
+            return ap[:, c * GROUP:(c + 1) * GROUP].rearrange("m (u p e) -> m u p e", u=2, e=2)
+
+        def natural(ap, c=0):
+            return ap[:, c * GROUP:(c + 1) * GROUP].rearrange("m (p u e) -> m u p e", u=2, e=2)
+
+        def part(size, half):
+            return slice(0, size) if half is None else slice(half * size // 2, (half + 1) * size // 2)
+
+        def tanh1(i, c, half=None):
+            if live(i):
+                u = part(2, half)
+                th = once("th", i, c, [P, GROUP], F32)
+                nc.scalar.activation(out=by_half(th)[:, u], in_=natural(t["a", i, c])[:, u], func=TANH)
+
+        def gain_mul(i, c, half=None):
+            if live(i):
+                u = part(2, half)
+                h = once("h", i, 0, [P, F], BF16)
+                nc.vector.tensor_tensor(out=by_half(h, c)[:, u], in0=by_half(t["th", i, c])[:, u],
+                                        in1=by_half(gain_all, c)[:, u], op=MULT)
+
+        def h_groups(b):
+            return 2 * b, min(2 * b + 2, GF)
+
+        def h_turn(i, b):
+            if not live(i):
+                return
+            words = t["h", i, 0][:].bitcast(F32)
+            g0, g1 = h_groups(b)
+            bank = turn.tile([P, g1 - g0, 2, P], F32, name="h_bank%d_%d" % (i, b), tag="h_bank%d" % b)
+            t["h_bank", i, b] = bank
+            for g in range(g0, g1):
+                for u in range(2):
+                    w0 = 256 * g + P * u
+                    nc.tensor.transpose(bank[:, g - g0, u, :], words[:, w0:w0 + P], ident[:])
+
+        def h_copy(i, b):
+            if live(i):
+                g0, g1 = h_groups(b)
+                interleave(once("h_rows", i, 0, [P, GF, P, 4], BF16)[:, g0:g1], t["h_bank", i, b][:])
+
+        def h_quant(i, b):
+            if live(i):
+                g0, g1 = h_groups(b)
+                codes = once("h_codes", i, 0, [P, GF * P], U32)
+                scales = once("h_scales", i, 0, [P, GF * P], U8)
+                quantize(codes[:, g0 * P:g1 * P], scales[:, g0 * P:g1 * P], t["h_rows", i, 0][:, g0:g1])
+
+        def mm2(i, c):
+            if not live(i):
+                return
+            acc = sums.tile([P, GROUP], F32, name="z%d_%d" % (i, c), tag="acc")
+            t["z", i, c] = acc
+            for g in range(GF):
+                nc.tensor.matmul_mx(
+                    out=acc[:],
+                    lhsT=t["h_codes", i, 0][:, g * P:(g + 1) * P].bitcast(FP8X4),
+                    lhsT_scale=t["h_scales", i, 0][:, g * P:(g + 1) * P],
+                    rhs=w2_sb[:, g, 2 * c * GROUP:2 * (c + 1) * GROUP].bitcast(FP4X4),
+                    rhs_scale=s2_sb[:, g, c * GROUP:(c + 1) * GROUP],
+                    start=(g == 0), stop=(g == GF - 1))
+
+        def bias_add(i, c, half=None):
+            if live(i):
+                cols = part(GROUP, half)
+                zb = once("zb", i, c, [P, GROUP], F32)
+                nc.vector.tensor_tensor(out=zb[:, cols], in0=t["z", i, c][:, cols],
+                                        in1=bias_all[:, c * GROUP:(c + 1) * GROUP][:, cols], op=ADD)
+
+        def tanh2(i, c, half=None):
+            if live(i):
+                cols = part(GROUP, half)
+                tz = once("tz", i, c, [P, GROUP], F32)
+                nc.scalar.activation(out=tz[:, cols], in_=t["zb", i, c][:, cols], func=TANH)
+
+        def weigh(i, c, half=None):
+            if live(i):
+                cols = part(GROUP, half)
+                y = once("y", i, c, [P, GROUP], F32)
+                nc.vector.tensor_tensor(out=y[:, cols], in0=t["tz", i, c][:, cols],
+                                        in1=rw_all[:, c * GROUP:(c + 1) * GROUP][:, cols], op=MULT)
+                if half != 0:
+                    nc.sync.dma_start(out=out_0[i * P:(i + 1) * P, c * GROUP:(c + 1) * GROUP], in_=y[:])
+
+        def y_round(i, c, half=None, on_scalar=False):
+            if live(i):
+                words = part(P, half)
+                y_bf = once("y_bf", i, c, [P, GROUP], BF16)
+                copy = nc.scalar.copy if on_scalar else nc.vector.tensor_copy
+                copy(out=by_half(y_bf)[:, :, words], in_=natural(t["y", i, c])[:, :, words])
+
+        def y_turn(i, groups=(0, 1), tag="y_bank"):
+            if not live(i):
+                return
+            bank = turn.tile([P, len(groups), 2, P], F32, name="y_bank%d_%d" % (i, groups[0]), tag=tag)
+            t["y_bank", i, groups[0]] = bank
+            for j, g in enumerate(groups):
+                words = t["y_bf", i, g][:].bitcast(F32)
+                for u in range(2):
+                    nc.tensor.transpose(bank[:, j, u, :], words[:, P * u:P * (u + 1)], ident[:])
+
+        def y_copy(i, groups=(0, 1)):
+            if live(i):
+                rows = once("y_rows", i, 0, [P, GN, P, 4], BF16)
+                interleave(rows[:, groups[0]:groups[-1] + 1], t["y_bank", i, groups[0]][:])
+
+        codes_hbm = out_1.rearrange("g p m t -> p g (m t)").bitcast(I32)
+
+        def y_quant(i, groups=(0, 1)):
+            if live(i):
+                tok = slice(i * P, (i + 1) * P)
+                for g in groups:
+                    quantize(y_codes[:, g, tok], y_scales[:, g, tok], t["y_rows", i, 0][:, g:g + 1])
+
+        def store_codes(i0, i1, g0=0, g1=GN):
+            span = slice(i0 * P, i1 * P)
+            nc.sync.dma_start(out=codes_hbm[:, g0:g1, span], in_=y_codes[:, g0:g1, span].bitcast(I32))
+
+        def store_scales(i0, i1):
+            span = slice(i0 * P, i1 * P)
+            for q in range(4):
+                nc.sync.dma_start(
+                    out=out_2[:, 4 * q:4 * q + 4, span].rearrange("g r m -> r g m").bitcast(I32),
+                    in_=y_scales[32 * q:32 * q + 4, :, span].bitcast(I32))
+
+        def spread(col, everywhere, j0, count, tag, in_order):
+            cols = col.bitcast(F32)
+            bank = turn.tile([P, count // 2, 2, P], F32, name="spread_bank", tag=tag)
+            for j in range(count):
+                nc.tensor.transpose(bank[:, j // 2, j % 2, :], cols[:, j0 + j:j0 + j + 1].to_broadcast([P, P]), ident[:])
+            words = everywhere[:].bitcast(F32)[:, j0 * P:(j0 + count) * P]
+            if in_order:
+                nc.vector.tensor_copy(out=words.rearrange("m (c p u) -> m c p u", p=P, u=2),
+                                      in_=bank[:].rearrange("m c u p -> m c p u"))
+            else:
+                nc.vector.tensor_copy(out=words, in_=bank[:].rearrange("m c u p -> m (c u p)"))
+
+        def first_layer(i, c):
+            mm1(i, c)
+            tanh1(i, c)
+            gain_mul(i, c)
+
+        gain_words = gain_col[:].rearrange("p c t -> p (c t)")
+        spread(gain_words, gain_all, 0, 4, "h_bank0", False)
+        spread(gain_words, gain_all, 4, 2, "h_bank1", False)
+        x_turn(0, ("x_bank0", "x_bank1", "y_bank", "h_bank0"))
+        for g in range(GD):
+            x_copy(0, g, 1)
+            x_quant(0, g, g + 1)
+        first_layer(0, 0)
+        x_turn(1)
+        spread(bias_col[:].rearrange("p c u e -> p (c u e)"), bias_all, 0, 4, "y_bank", True)
+        spread(rw_col[:].rearrange("p c u e -> p (c u e)"), rw_all, 0, 4, "h_bank0", True)
+        for b in range(2):
+            x_copy(1, b)
+            x_quant(1, 2 * b, 2 * b + 2)
+        first_layer(0, 1)
+        first_layer(1, 0)
+        first_layer(0, 2)
+        first_layer(1, 1)
+        x_turn(2)
+        h_turn(0, 0)
+        h_turn(0, 1)
+        x_copy(2, 0)
+        for b in range(2):
+            h_copy(0, b)
+            h_quant(0, b)
+        x_copy(2, 1)
+        mm1(1, 2)
+        mm2(0, 0)
+        tanh1(1, 2)
+        x_quant(2, 0, GD)
+        gain_mul(1, 2)
+        mm2(0, 1)
+        bias_add(0, 0)
+
+        last = TILES - 1
+        for i in range(2, last):
+            x_turn(i + 1)
+            bias_add(i - 2, 1)
+            tanh2(i - 2, 0)
+            x_copy(i + 1, 0)
+            weigh(i - 2, 0)
+            tanh2(i - 2, 1)
+            y_turn(i - 3)
+            h_turn(i - 1, 0)
+            h_turn(i - 1, 1)
+            x_copy(i + 1, 1)
+            weigh(i - 2, 1)
+            y_round(i - 2, 0)
+            mm1(i, 0)
+            h_copy(i - 1, 0)
+            h_copy(i - 1, 1)
+            x_quant(i + 1, 0, GD)
+            y_round(i - 2, 1)
+            y_copy(i - 3)
+            h_quant(i - 1, 0)
+            h_quant(i - 1, 1)
+            y_quant(i - 3)
+            if i - 3 in (1, 3):
+                store_codes(i - 4, i - 2)
+            mm1(i, 1)
+            tanh1(i, 0)
+            gain_mul(i, 0)
+            mm1(i, 2)
+            tanh1(i, 1)
+            gain_mul(i, 1)
+            mm2(i - 1, 0)
+            tanh1(i, 2)
+            gain_mul(i, 2)
+            mm2(i - 1, 1)
+            bias_add(i - 1, 0)
+
+        bias_add(5, 1)
+        tanh2(5, 0)
+        weigh(5, 0)
+        tanh2(5, 1)
+        y_turn(4)
+        h_turn(6, 0)
+        h_turn(6, 1)
+        weigh(5, 1)
+        y_round(5, 0)
+        mm1(7, 0)
+        h_copy(6, 0)
+        h_copy(6, 1)
+        h_quant(6, 0)
+        h_quant(6, 1)
+        y_round(5, 1)
+        mm1(7, 1)
+        tanh1(7, 0)
+        gain_mul(7, 0)
+        mm1(7, 2)
+        tanh1(7, 1)
+        gain_mul(7, 1)
+        y_copy(4)
+        y_quant(4)
+        store_codes(4, 5)
+        store_scales(0, 5)
+        mm2(6, 0)
+        tanh1(7, 2, 0)
+        tanh1(7, 2, 1)
+        gain_mul(7, 2, 0)
+        gain_mul(7, 2, 1)
+        h_turn(7, 0)
+        mm2(6, 1)
+        bias_add(6, 0)
+        h_copy(7, 0)
+        h_quant(7, 0)
+        h_turn(7, 1)
+        y_turn(5)
+        tanh2(6, 0)
+        h_copy(7, 1)
+        bias_add(6, 1)
+        h_quant(7, 1)
+        mm2(7, 0)
+        mm2(7, 1)
+        weigh(6, 0)
+        tanh2(6, 1)
+        y_copy(5)
+        bias_add(7, 0)
+        y_round(6, 0, None, True)
+        weigh(6, 1)
+        tanh2(7, 0)
+        bias_add(7, 1, 0)
+        bias_add(7, 1, 1)
+        tanh2(7, 1, 0)
+        tanh2(7, 1, 1)
+        weigh(7, 0)
+        y_round(6, 1, None, True)
+        y_turn(6)
+        weigh(7, 1, 0)
+        weigh(7, 1, 1)
+        y_round(7, 0)
+        y_turn(7, (0,), "x_bank0")
+        y_round(7, 1, 0)
+        y_round(7, 1, 1)
+        y_turn(7, (1,), "x_bank1")
+        y_copy(6)
+        y_quant(5)
+        y_copy(7, (0,))
+        y_copy(7, (1,))
+        y_quant(6)
+        store_codes(5, 7)
+        y_quant(7, (0,))
+        y_quant(7, (1,))
+        store_codes(7, 8)
+        store_scales(5, 8)

@@ -28,7 +28,7 @@ def tile_reward_head_terms_h1_kernel(tc, x, w1_words, w1_scales, gain, w2_words,
     nc = tc.nc
     with ExitStack() as ctx:
         keep = ctx.enter_context(tc.tile_pool(name="keep", bufs=1))
-        work = ctx.enter_context(tc.tile_pool(name="work", bufs=4))
+        work = ctx.enter_context(tc.tile_pool(name="work", bufs=3))
         turn = ctx.enter_context(tc.psum_pool(name="turn", bufs=1))
         sums = ctx.enter_context(tc.psum_pool(name="sums", bufs=3))
         ctx.enter_context(tc.manual_schedule())
@@ -41,12 +41,13 @@ def tile_reward_head_terms_h1_kernel(tc, x, w1_words, w1_scales, gain, w2_words,
         s1_sb = [keep.tile([P, GD, GROUP], U8, name="s1_sb%d" % c, align_bytes=64) for c in range(GF)]
         w2_sb = keep.tile([P, GF, 2 * N], U8, name="w2_sb", align_bytes=64)
         s2_sb = keep.tile([P, GF, N], U8, name="s2_sb", align_bytes=64)
-        gain_col = keep.tile([P, GF, 4], BF16, name="gain_col", align_bytes=64)
-        bias_col = keep.tile([P, GN, 2, 2], BF16, name="bias_col", align_bytes=64)
-        rw_col = keep.tile([P, GN, 2, 2], BF16, name="rw_col", align_bytes=64)
         gain_all = keep.tile([P, F], BF16, name="gain_all", align_bytes=64)
-        bias_all = keep.tile([P, N], BF16, name="bias_all", align_bytes=64)
-        rw_all = keep.tile([P, N], BF16, name="rw_all", align_bytes=64)
+        vectors = {"gain": gain, "bias": bias, "rw": reward_weight}
+        column = {k: keep.tile([P, v.shape[0] // 32], BF16, name=k + "_column", align_bytes=64) for k, v in vectors.items()}
+        wide = {k: keep.tile([P, v.shape[0] // 2], F32, name=k + "_wide", align_bytes=64) for k, v in vectors.items()}
+        turned = {k: keep.tile([P, v.shape[0] // 2], F32, name=k + "_turned", align_bytes=64) for k, v in vectors.items()}
+        spread = {k: keep.tile([P, v.shape[0]], BF16, name=k + "_spread", align_bytes=64) for k, v in vectors.items()}
+        bias_all, rw_all = spread["bias"], spread["rw"]
         y_codes = keep.tile([P, GN, M], U32, name="y_codes", align_bytes=64)
         y_scales = keep.tile([P, GN, M], U8, name="y_scales", align_bytes=64)
         warm = keep.tile([P, 2], F32, name="warm", align_bytes=64)
@@ -73,14 +74,17 @@ def tile_reward_head_terms_h1_kernel(tc, x, w1_words, w1_scales, gain, w2_words,
                     out=w1_sb[c][:, g:g + step, :].bitcast(I32),
                     in_=w1_words[g:g + step, :, 2 * c * GROUP:2 * (c + 1) * GROUP].rearrange("g p b -> p g b").bitcast(I32))
 
-        nc.scalar.dma_start(out=gain_col[:], in_=gain.rearrange("(c p t) -> p c t", p=P, t=4))
+        def load_vector(queue, k):
+            queue.dma_start(out=column[k][:], in_=vectors[k].rearrange("(r b) -> r b", r=32).partition_broadcast(4))
+
+        load_vector(nc.scalar, "gain")
         nc.scalar.activation(out=warm[:, 1:2], in_=warm[:, 0:1], func=TANH)
         load_x(0, 0, D // 2)
         load_x(0, D // 2, D)
         load_w1(0, 2)
         load_x(1, 0, D)
-        nc.sync.dma_start(out=bias_col[:].rearrange("p c u e -> p c (u e)"), in_=bias.rearrange("(c p t) -> p c t", p=P, t=4))
-        nc.sync.dma_start(out=rw_col[:].rearrange("p c u e -> p c (u e)"), in_=reward_weight.rearrange("(c p t) -> p c t", p=P, t=4))
+        load_vector(nc.sync, "bias")
+        load_vector(nc.sync, "rw")
         load_w1(1, 1)
         load_w1(2, 1)
         load_x(2, 0, D)
@@ -94,18 +98,27 @@ def tile_reward_head_terms_h1_kernel(tc, x, w1_words, w1_scales, gain, w2_words,
         def live(i):
             return 0 <= i < TILES
 
+        def x_sort(i, b, on_vector=False):
+            if live(i):
+                x_sorted = once("x_sorted", i, 0, [P, GD, 2, P], F32)
+                words = x_sb[i][:].bitcast(F32).rearrange("m (g p u) -> m g u p", g=GD, u=2)
+                copy = nc.vector.tensor_copy if on_vector else nc.scalar.copy
+                copy(out=x_sorted[:, 2 * b:2 * b + 2], in_=words[:, 2 * b:2 * b + 2])
+
         def x_turn(i, tags=("x_bank0", "x_bank1")):
             if not live(i):
                 return
-            words = x_sb[i][:].bitcast(F32)
+            if i == 0:
+                words = x_sb[i][:].bitcast(F32).rearrange("m (g p u) -> m g u p", g=GD, u=2)
+            else:
+                words = t["x_sorted", i, 0]
             groups = GD // len(tags)
             for b, tag in enumerate(tags):
                 bank = turn.tile([P, groups, 2, P], F32, name="x_bank%d_%d" % (i, b), tag=tag)
                 t["x_bank", i, b] = bank
                 for g in range(groups):
                     for u in range(2):
-                        w0 = 256 * (groups * b + g)
-                        nc.tensor.transpose(bank[:, g, u, :], words[:, w0 + u:w0 + 256:2], ident[:])
+                        nc.tensor.transpose(bank[:, g, u, :], words[:, groups * b + g, u, :], ident[:])
             t["x_rows", i] = work.tile([P, GD, P, 4], BF16, name="x_rows%d" % i, tag="x_rows", align_bytes=64)
             t["x_codes", i] = work.tile([P, GD * P], U32, name="x_codes%d" % i, tag="x_codes", align_bytes=64)
             t["x_scales", i] = work.tile([P, GD * P], U8, name="x_scales%d" % i, tag="x_scales", align_bytes=64)
@@ -140,7 +153,8 @@ def tile_reward_head_terms_h1_kernel(tc, x, w1_words, w1_scales, gain, w2_words,
 
         def once(kind, i, c, shape, dtype):
             if (kind, i, c) not in t:
-                t[kind, i, c] = work.tile(shape, dtype, name="%s%d_%d" % (kind, i, c), tag=kind, align_bytes=64)
+                t[kind, i, c] = work.tile(shape, dtype, name="%s%d_%d" % (kind, i, c), tag=kind, align_bytes=64,
+                                          bufs=4 if kind == "th" else 3)
             return t[kind, i, c]
 
         def by_half(ap, c=0):
@@ -206,34 +220,41 @@ def tile_reward_head_terms_h1_kernel(tc, x, w1_words, w1_scales, gain, w2_words,
                     rhs_scale=s2_sb[:, g, c * GROUP:(c + 1) * GROUP],
                     start=(g == 0), stop=(g == GF - 1))
 
+        def span(c, half):
+            if c is None:
+                return slice(0, N)
+            cols = part(GROUP, half)
+            return slice(c * GROUP + cols.start, c * GROUP + cols.stop)
+
         def bias_add(i, c, half=None):
             if live(i):
-                cols = part(GROUP, half)
-                zb = once("zb", i, c, [P, GROUP], F32)
-                nc.vector.tensor_tensor(out=zb[:, cols], in0=t["z", i, c][:, cols],
-                                        in1=bias_all[:, c * GROUP:(c + 1) * GROUP][:, cols], op=ADD)
+                zb = once("zb", i, 0, [P, N], F32)
+                nc.vector.tensor_tensor(out=zb[:, span(c, half)], in0=t["z", i, c][:, part(GROUP, half)],
+                                        in1=bias_all[:, span(c, half)], op=ADD)
 
-        def tanh2(i, c, half=None):
+        def tanh2(i, c=None, half=None):
             if live(i):
-                cols = part(GROUP, half)
-                tz = once("tz", i, c, [P, GROUP], F32)
-                nc.scalar.activation(out=tz[:, cols], in_=t["zb", i, c][:, cols], func=TANH)
+                cols = span(c, half)
+                tz = once("tz", i, 0, [P, N], F32)
+                nc.scalar.activation(out=tz[:, cols], in_=t["zb", i, 0][:, cols], func=TANH)
 
-        def weigh(i, c, half=None):
+        def weigh(i, c=None, half=None):
             if live(i):
-                cols = part(GROUP, half)
-                y = once("y", i, c, [P, GROUP], F32)
-                nc.vector.tensor_tensor(out=y[:, cols], in0=t["tz", i, c][:, cols],
-                                        in1=rw_all[:, c * GROUP:(c + 1) * GROUP][:, cols], op=MULT)
-                if half != 0:
-                    nc.sync.dma_start(out=out_0[i * P:(i + 1) * P, c * GROUP:(c + 1) * GROUP], in_=y[:])
+                cols = span(c, half)
+                y = once("y", i, 0, [P, N], F32)
+                nc.vector.tensor_tensor(out=y[:, cols], in0=t["tz", i, 0][:, cols], in1=rw_all[:, cols], op=MULT)
+
+        def store_y(i, c=None):
+            if live(i):
+                cols = span(c, None)
+                nc.sync.dma_start(out=out_0[i * P:(i + 1) * P, cols], in_=t["y", i, 0][:, cols])
 
         def y_round(i, c, half=None, on_scalar=False):
             if live(i):
                 words = part(P, half)
-                y_bf = once("y_bf", i, c, [P, GROUP], BF16)
+                y_bf = once("y_bf", i, 0, [P, N], BF16)
                 copy = nc.scalar.copy if on_scalar else nc.vector.tensor_copy
-                copy(out=by_half(y_bf)[:, :, words], in_=natural(t["y", i, c])[:, :, words])
+                copy(out=by_half(y_bf, c)[:, :, words], in_=natural(t["y", i, 0], c)[:, :, words])
 
         def y_turn(i, groups=(0, 1), tag="y_bank"):
             if not live(i):
@@ -241,7 +262,7 @@ def tile_reward_head_terms_h1_kernel(tc, x, w1_words, w1_scales, gain, w2_words,
             bank = turn.tile([P, len(groups), 2, P], F32, name="y_bank%d_%d" % (i, groups[0]), tag=tag)
             t["y_bank", i, groups[0]] = bank
             for j, g in enumerate(groups):
-                words = t["y_bf", i, g][:].bitcast(F32)
+                words = t["y_bf", i, 0][:, g * GROUP:(g + 1) * GROUP].bitcast(F32)
                 for u in range(2):
                     nc.tensor.transpose(bank[:, j, u, :], words[:, P * u:P * (u + 1)], ident[:])
 
@@ -262,6 +283,10 @@ def tile_reward_head_terms_h1_kernel(tc, x, w1_words, w1_scales, gain, w2_words,
             span = slice(i0 * P, i1 * P)
             nc.sync.dma_start(out=codes_hbm[:, g0:g1, span], in_=y_codes[:, g0:g1, span].bitcast(I32))
 
+        def store_pair(i):
+            if i in (1, 3):
+                store_codes(i - 1, i + 1)
+
         def store_scales(i0, i1):
             span = slice(i0 * P, i1 * P)
             for q in range(4):
@@ -269,163 +294,201 @@ def tile_reward_head_terms_h1_kernel(tc, x, w1_words, w1_scales, gain, w2_words,
                     out=out_2[:, 4 * q:4 * q + 4, span].rearrange("g r m -> r g m").bitcast(I32),
                     in_=y_scales[32 * q:32 * q + 4, :, span].bitcast(I32))
 
-        def spread(col, everywhere, j0, count, tag, in_order):
-            cols = col.bitcast(F32)
-            bank = turn.tile([P, count // 2, 2, P], F32, name="spread_bank", tag=tag)
-            for j in range(count):
-                nc.tensor.transpose(bank[:, j // 2, j % 2, :], cols[:, j0 + j:j0 + j + 1].to_broadcast([P, P]), ident[:])
-            words = everywhere[:].bitcast(F32)[:, j0 * P:(j0 + count) * P]
-            if in_order:
-                nc.vector.tensor_copy(out=words.rearrange("m (c p u) -> m c p u", p=P, u=2),
-                                      in_=bank[:].rearrange("m c u p -> m c p u"))
-            else:
-                nc.vector.tensor_copy(out=words, in_=bank[:].rearrange("m c u p -> m (c u p)"))
+        def widen(k):
+            words = column[k][:].bitcast(F32)
+            nc.vector.tensor_copy(out=wide[k][:].rearrange("m (b j) -> m b j", j=32),
+                                  in_=words.unsqueeze(2).to_broadcast([P, words.shape[1], 32]))
+
+        def turn_blocks(k):
+            nc.vector.transpose(out=turned[k][:], in_=wide[k][:])
+
+        def put_in_order(k):
+            nc.scalar.copy(out=spread[k][:].bitcast(F32).rearrange("m (r b) -> m r b", r=32),
+                           in_=turned[k][:].rearrange("m (b r) -> m r b", r=32))
+
+        def sort_gain():
+            nc.scalar.copy(out=gain_all[:].bitcast(F32).rearrange("m (c u p) -> m c u p", c=GF, u=2),
+                           in_=spread["gain"][:].bitcast(F32).rearrange("m (c p u) -> m c u p", c=GF, u=2))
 
         def first_layer(i, c):
             mm1(i, c)
             tanh1(i, c)
             gain_mul(i, c)
 
-        gain_words = gain_col[:].rearrange("p c t -> p (c t)")
-        spread(gain_words, gain_all, 0, 4, "h_bank0", False)
-        spread(gain_words, gain_all, 4, 2, "h_bank1", False)
         x_turn(0, ("x_bank0", "x_bank1", "y_bank", "h_bank0"))
-        for g in range(GD):
-            x_copy(0, g, 1)
-            x_quant(0, g, g + 1)
-        first_layer(0, 0)
+        widen("gain")
+        turn_blocks("gain")
+        x_copy(0, 0, 1)
+        x_copy(0, 1, 1)
+        x_copy(0, 2, 1)
+        x_copy(0, 3, 1)
+        x_quant(0, 0, 1)
+        x_quant(0, 1, 2)
+        x_quant(0, 3, 4)
+        x_quant(0, 2, 3)
+        widen("rw")
+        x_sort(1, 0, True)
+        x_sort(1, 1, True)
+        mm1(0, 0)
+        widen("bias")
+        put_in_order("gain")
+        turn_blocks("bias")
+        sort_gain()
+        tanh1(0, 0)
         x_turn(1)
-        spread(bias_col[:].rearrange("p c u e -> p (c u e)"), bias_all, 0, 4, "y_bank", True)
-        spread(rw_col[:].rearrange("p c u e -> p (c u e)"), rw_all, 0, 4, "h_bank0", True)
-        for b in range(2):
-            x_copy(1, b)
-            x_quant(1, 2 * b, 2 * b + 2)
-        first_layer(0, 1)
-        first_layer(1, 0)
-        first_layer(0, 2)
-        first_layer(1, 1)
-        x_turn(2)
+        x_copy(1, 0)
+        x_quant(1, 0, 2)
+        x_copy(1, 1)
+        mm1(0, 1)
+        x_quant(1, 2, 4)
+        mm1(1, 0)
+        tanh1(0, 1)
+        gain_mul(0, 0)
+        put_in_order("bias")
+        mm1(0, 2)
+        gain_mul(0, 1)
+        x_sort(2, 0, True)
+        tanh1(1, 0)
+        turn_blocks("rw")
+        mm1(1, 1)
+        tanh1(0, 2)
+        x_sort(2, 1, True)
+        tanh1(1, 1)
         h_turn(0, 0)
+        x_turn(2)
+        gain_mul(0, 2)
+        h_copy(0, 0)
         h_turn(0, 1)
-        x_copy(2, 0)
-        for b in range(2):
-            h_copy(0, b)
-            h_quant(0, b)
         x_copy(2, 1)
+        h_copy(0, 1)
+        x_copy(2, 0)
         mm1(1, 2)
+        gain_mul(1, 0)
+        h_quant(0, 0)
+        gain_mul(1, 1)
+        h_quant(0, 1)
         mm2(0, 0)
-        tanh1(1, 2)
+        x_sort(3, 1, True)
+        x_sort(3, 0)
         x_quant(2, 0, GD)
-        gain_mul(1, 2)
-        mm2(0, 1)
         bias_add(0, 0)
+        tanh1(1, 2)
+        put_in_order("rw")
+        mm2(0, 1)
+        gain_mul(1, 2)
 
         last = TILES - 1
         for i in range(2, last):
-            x_turn(i + 1)
-            bias_add(i - 2, 1)
             tanh2(i - 2, 0)
-            x_copy(i + 1, 0)
-            weigh(i - 2, 0)
-            tanh2(i - 2, 1)
-            y_turn(i - 3)
+            bias_add(i - 2, 1)
+            x_turn(i + 1)
             h_turn(i - 1, 0)
+            weigh(i - 2, 0)
             h_turn(i - 1, 1)
-            x_copy(i + 1, 1)
-            weigh(i - 2, 1)
-            y_round(i - 2, 0)
+            y_turn(i - 3)
+            x_copy(i + 1, 0)
             mm1(i, 0)
-            h_copy(i - 1, 0)
             h_copy(i - 1, 1)
-            x_quant(i + 1, 0, GD)
-            y_round(i - 2, 1)
-            y_copy(i - 3)
-            h_quant(i - 1, 0)
+            tanh2(i - 2, 1)
+            x_sort(i + 2, 1, True)
+            x_copy(i + 1, 1)
+            h_copy(i - 1, 0)
             h_quant(i - 1, 1)
-            y_quant(i - 3)
-            if i - 3 in (1, 3):
-                store_codes(i - 4, i - 2)
+            y_round(i - 2, 0)
             mm1(i, 1)
+            y_copy(i - 3)
             tanh1(i, 0)
-            gain_mul(i, 0)
+            weigh(i - 2, 1)
+            x_quant(i + 1, 0, GD)
+            h_quant(i - 1, 0)
             mm1(i, 2)
+            y_round(i - 2, 1)
             tanh1(i, 1)
-            gain_mul(i, 1)
-            mm2(i - 1, 0)
+            store_y(i - 2)
             tanh1(i, 2)
+            mm2(i - 1, 0)
+            y_quant(i - 3)
+            gain_mul(i, 0)
+            gain_mul(i, 1)
+            x_sort(i + 2, 0)
+            store_pair(i - 3)
+            bias_add(i - 1, 0)
             gain_mul(i, 2)
             mm2(i - 1, 1)
-            bias_add(i - 1, 0)
 
+        mm1(7, 0)
+        h_turn(6, 0)
         bias_add(5, 1)
         tanh2(5, 0)
-        weigh(5, 0)
-        tanh2(5, 1)
+        tanh1(7, 0)
         y_turn(4)
-        h_turn(6, 0)
-        h_turn(6, 1)
-        weigh(5, 1)
+        weigh(5, 0)
         y_round(5, 0)
-        mm1(7, 0)
+        h_turn(6, 1)
+        tanh2(5, 1)
         h_copy(6, 0)
-        h_copy(6, 1)
+        gain_mul(7, 0)
+        weigh(5, 1)
         h_quant(6, 0)
+        h_copy(6, 1)
+        mm1(7, 1)
+        tanh1(7, 1)
+        y_copy(4)
+        mm1(7, 2)
         h_quant(6, 1)
         y_round(5, 1)
-        mm1(7, 1)
-        tanh1(7, 0)
-        gain_mul(7, 0)
-        mm1(7, 2)
-        tanh1(7, 1)
-        gain_mul(7, 1)
-        y_copy(4)
-        y_quant(4)
-        store_codes(4, 5)
-        store_scales(0, 5)
         mm2(6, 0)
         tanh1(7, 2, 0)
         tanh1(7, 2, 1)
+        gain_mul(7, 1)
+        store_y(5)
         gain_mul(7, 2, 0)
-        gain_mul(7, 2, 1)
         h_turn(7, 0)
-        mm2(6, 1)
-        bias_add(6, 0)
         h_copy(7, 0)
+        gain_mul(7, 2, 1)
+        bias_add(6, 0)
+        y_turn(5)
         h_quant(7, 0)
         h_turn(7, 1)
-        y_turn(5)
-        tanh2(6, 0)
+        y_quant(4)
         h_copy(7, 1)
-        bias_add(6, 1)
+        mm2(6, 1)
+        tanh2(6, 0)
         h_quant(7, 1)
         mm2(7, 0)
+        y_copy(5)
+        bias_add(6, 1)
         mm2(7, 1)
         weigh(6, 0)
-        tanh2(6, 1)
-        y_copy(5)
         bias_add(7, 0)
-        y_round(6, 0, None, True)
-        weigh(6, 1)
-        tanh2(7, 0)
+        tanh2(6, 1)
         bias_add(7, 1, 0)
+        y_round(6, 0, None, True)
+        tanh2(7, 0)
         bias_add(7, 1, 1)
+        weigh(6, 1)
         tanh2(7, 1, 0)
-        tanh2(7, 1, 1)
         weigh(7, 0)
+        weigh(7, 1, 0)
+        store_codes(4, 5)
+        tanh2(7, 1, 1)
         y_round(6, 1, None, True)
         y_turn(6)
-        weigh(7, 1, 0)
         weigh(7, 1, 1)
+        y_copy(6)
         y_round(7, 0)
         y_turn(7, (0,), "x_bank0")
+        store_scales(0, 5)
+        store_y(6)
+        y_copy(7, (0,))
         y_round(7, 1, 0)
         y_round(7, 1, 1)
-        y_turn(7, (1,), "x_bank1")
-        y_copy(6)
         y_quant(5)
-        y_copy(7, (0,))
-        y_copy(7, (1,))
+        store_y(7, 0)
         y_quant(6)
+        y_turn(7, (1,), "x_bank1")
+        y_copy(7, (1,))
+        store_y(7, 1)
         store_codes(5, 7)
         y_quant(7, (0,))
         y_quant(7, (1,))

@@ -61,10 +61,10 @@ def tile_reward_head_terms_h1_kernel(tc, x, w1_words, w1_scales, gain, w2_words,
             nc.sync.dma_start(out=x_sb[i][:, k0:k1], in_=x[i * P:(i + 1) * P, k0:k1])
 
         def load_scales(plane, rows, n0, n1):
-            for q in range(4):
+            for r in range(4):
                 nc.sync.dma_start(
-                    out=plane[32 * q:32 * q + 4].bitcast(I32),
-                    in_=rows[:, 4 * q:4 * q + 4, n0:n1].rearrange("g r n -> r g n").bitcast(I32))
+                    out=plane[r:P:32].bitcast(I32),
+                    in_=rows[:, r:16:4, n0:n1].rearrange("g q n -> q g n").bitcast(I32))
 
         def load_w1(c, pieces):
             load_scales(s1_sb[c], w1_scales, c * GROUP, (c + 1) * GROUP)
@@ -289,10 +289,10 @@ def tile_reward_head_terms_h1_kernel(tc, x, w1_words, w1_scales, gain, w2_words,
 
         def store_scales(i0, i1):
             span = slice(i0 * P, i1 * P)
-            for q in range(4):
+            for r in range(4):
                 nc.sync.dma_start(
-                    out=out_2[:, 4 * q:4 * q + 4, span].rearrange("g r m -> r g m").bitcast(I32),
-                    in_=y_scales[32 * q:32 * q + 4, :, span].bitcast(I32))
+                    out=out_2[:, r:16:4, span].rearrange("g q m -> q g m").bitcast(I32),
+                    in_=y_scales[r:P:32, :, span].bitcast(I32))
 
         def widen(k):
             words = column[k][:].bitcast(F32)

@@ -101,9 +101,9 @@ def tile_reward_head_terms_h1_kernel(tc, x, w1_words, w1_scales, gain, w2_words,
         def x_sort(i, b, on_vector=False):
             if live(i):
                 x_sorted = once("x_sorted", i, 0, [P, GD, 2, P], F32)
-                words = x_sb[i][:].bitcast(F32).rearrange("m (g p u) -> m g u p", g=GD, u=2)
+                words = x_sb[i][:].bitcast(F32).rearrange("m (g p u) -> m g p u", g=GD, u=2)
                 copy = nc.vector.tensor_copy if on_vector else nc.scalar.copy
-                copy(out=x_sorted[:, 2 * b:2 * b + 2], in_=words[:, 2 * b:2 * b + 2])
+                copy(out=x_sorted[:, 2 * b:2 * b + 2].rearrange("m g u p -> m g p u"), in_=words[:, 2 * b:2 * b + 2])
 
         def x_turn(i, tags=("x_bank0", "x_bank1")):
             if not live(i):
@@ -287,10 +287,10 @@ def tile_reward_head_terms_h1_kernel(tc, x, w1_words, w1_scales, gain, w2_words,
             if i in (1, 3):
                 store_codes(i - 1, i + 1)
 
-        def store_scales(i0, i1):
+        def store_scales(i0, i1, queue):
             span = slice(i0 * P, i1 * P)
             for r in range(4):
-                nc.sync.dma_start(
+                queue.dma_start(
                     out=out_2[:, r:16:4, span].rearrange("g q m -> q g m").bitcast(I32),
                     in_=y_scales[r:P:32, :, span].bitcast(I32))
 
@@ -478,7 +478,7 @@ def tile_reward_head_terms_h1_kernel(tc, x, w1_words, w1_scales, gain, w2_words,
         y_copy(6)
         y_round(7, 0)
         y_turn(7, (0,), "x_bank0")
-        store_scales(0, 5)
+        store_scales(0, 5, nc.sync)
         store_y(6)
         y_copy(7, (0,))
         y_round(7, 1, 0)
@@ -493,4 +493,4 @@ def tile_reward_head_terms_h1_kernel(tc, x, w1_words, w1_scales, gain, w2_words,
         y_quant(7, (0,))
         y_quant(7, (1,))
         store_codes(7, 8)
-        store_scales(5, 8)
+        store_scales(5, 8, nc.scalar)

@@ -18,9 +18,16 @@ ADD = mybir.AluOpType.add
 MULT = mybir.AluOpType.mult
 
 P = 128
+QUAD = 32
 GROUP = 512
+PAIRS = GROUP // 2
+SCALE_ROWS = GROUP // 32
 TILES = M // P
 GD, GF, GN = D // GROUP, F // GROUP, N // GROUP
+ALIGN = 64
+WORK_BUFS = 3
+TANH_BUFS = 4
+SUM_BANKS = 3
 
 
 def tile_reward_head_terms_h1_kernel(tc, x, w1_words, w1_scales, gain, w2_words, w2_scales, bias,
@@ -28,34 +35,36 @@ def tile_reward_head_terms_h1_kernel(tc, x, w1_words, w1_scales, gain, w2_words,
     nc = tc.nc
     with ExitStack() as ctx:
         keep = ctx.enter_context(tc.tile_pool(name="keep", bufs=1))
-        work = ctx.enter_context(tc.tile_pool(name="work", bufs=3))
+        work = ctx.enter_context(tc.tile_pool(name="work", bufs=WORK_BUFS))
         turn = ctx.enter_context(tc.psum_pool(name="turn", bufs=1))
-        sums = ctx.enter_context(tc.psum_pool(name="sums", bufs=3))
+        sums = ctx.enter_context(tc.psum_pool(name="sums", bufs=SUM_BANKS))
         ctx.enter_context(tc.manual_schedule())
 
-        ident = keep.tile([P, P], F32, name="ident", align_bytes=64)
+        ident = keep.tile([P, P], F32, name="ident", align_bytes=ALIGN)
         make_identity(nc, ident[:])
 
-        x_sb = [keep.tile([P, D], BF16, name="x_sb%d" % i, align_bytes=64) for i in range(TILES)]
-        w1_sb = [keep.tile([P, GD, 2 * GROUP], U8, name="w1_sb%d" % c, align_bytes=64) for c in range(GF)]
-        s1_sb = [keep.tile([P, GD, GROUP], U8, name="s1_sb%d" % c, align_bytes=64) for c in range(GF)]
-        w2_sb = keep.tile([P, GF, 2 * N], U8, name="w2_sb", align_bytes=64)
-        s2_sb = keep.tile([P, GF, N], U8, name="s2_sb", align_bytes=64)
-        gain_all = keep.tile([P, F], BF16, name="gain_all", align_bytes=64)
-        vectors = {"gain": gain, "bias": bias, "rw": reward_weight}
-        column = {k: keep.tile([P, v.shape[0] // 32], BF16, name=k + "_column", align_bytes=64) for k, v in vectors.items()}
-        wide = {k: keep.tile([P, v.shape[0] // 2], F32, name=k + "_wide", align_bytes=64) for k, v in vectors.items()}
-        turned = {k: keep.tile([P, v.shape[0] // 2], F32, name=k + "_turned", align_bytes=64) for k, v in vectors.items()}
-        spread = {k: keep.tile([P, v.shape[0]], BF16, name=k + "_spread", align_bytes=64) for k, v in vectors.items()}
-        bias_all, rw_all = spread["bias"], spread["rw"]
-        y_codes = keep.tile([P, GN, M], U32, name="y_codes", align_bytes=64)
-        y_scales = keep.tile([P, GN, M], U8, name="y_scales", align_bytes=64)
-        warm = keep.tile([P, 2], F32, name="warm", align_bytes=64)
+        x_sb = [keep.tile([P, D], BF16, name="x_sb%d" % i, align_bytes=ALIGN) for i in range(TILES)]
+        w1_sb = [keep.tile([P, GD, 2 * GROUP], U8, name="w1_sb%d" % c, align_bytes=ALIGN) for c in range(GF)]
+        s1_sb = [keep.tile([P, GD, GROUP], U8, name="s1_sb%d" % c, align_bytes=ALIGN) for c in range(GF)]
+        w2_sb = keep.tile([P, GF, 2 * N], U8, name="w2_sb", align_bytes=ALIGN)
+        s2_sb = keep.tile([P, GF, N], U8, name="s2_sb", align_bytes=ALIGN)
+        gain_sorted = keep.tile([P, F], BF16, name="gain_sorted", align_bytes=ALIGN)
+        vectors = {"gain": gain, "bias": bias, "weight": reward_weight}
+        column = {k: keep.tile([P, v.shape[0] // QUAD], BF16, name=k + "_column", align_bytes=ALIGN)
+                  for k, v in vectors.items()}
+        wide = {k: keep.tile([P, v.shape[0] // 2], F32, name=k + "_wide", align_bytes=ALIGN)
+                for k, v in vectors.items()}
+        turned = {k: keep.tile([P, v.shape[0] // 2], F32, name=k + "_turned", align_bytes=ALIGN)
+                  for k, v in vectors.items()}
+        spread = {k: keep.tile([P, v.shape[0]], BF16, name=k + "_spread", align_bytes=ALIGN)
+                  for k, v in vectors.items()}
+        y_codes = keep.tile([P, GN, M], U32, name="y_codes", align_bytes=ALIGN)
+        y_scales = keep.tile([P, GN, M], U8, name="y_scales", align_bytes=ALIGN)
 
         for c in range(GF):
             nc.vector.memset(s1_sb[c][:].rearrange("p g n -> p (g n)").bitcast(I32), 0)
         nc.vector.memset(s2_sb[:].rearrange("p g n -> p (g n)").bitcast(I32), 0)
-        nc.gpsimd.memset(warm[:, 0:1], 0.0)
+
 
         def load_x(i, k0, k1):
             nc.sync.dma_start(out=x_sb[i][:, k0:k1], in_=x[i * P:(i + 1) * P, k0:k1])
@@ -63,28 +72,28 @@ def tile_reward_head_terms_h1_kernel(tc, x, w1_words, w1_scales, gain, w2_words,
         def load_scales(plane, rows, n0, n1):
             for r in range(4):
                 nc.sync.dma_start(
-                    out=plane[r:P:32].bitcast(I32),
-                    in_=rows[:, r:16:4, n0:n1].rearrange("g q n -> q g n").bitcast(I32))
+                    out=plane[r:P:QUAD].bitcast(I32),
+                    in_=rows[:, r:SCALE_ROWS:4, n0:n1].rearrange("g q n -> q g n").bitcast(I32))
 
         def load_w1(c, pieces):
             load_scales(s1_sb[c], w1_scales, c * GROUP, (c + 1) * GROUP)
             step = GD // pieces
             for g in range(0, GD, step):
-                nc.sync.dma_start(
-                    out=w1_sb[c][:, g:g + step, :].bitcast(I32),
-                    in_=w1_words[g:g + step, :, 2 * c * GROUP:2 * (c + 1) * GROUP].rearrange("g p b -> p g b").bitcast(I32))
+                words = w1_words[g:g + step, :, 2 * c * GROUP:2 * (c + 1) * GROUP]
+                nc.sync.dma_start(out=w1_sb[c][:, g:g + step, :].bitcast(I32),
+                                  in_=words.rearrange("g p b -> p g b").bitcast(I32))
 
         def load_vector(queue, k):
-            queue.dma_start(out=column[k][:], in_=vectors[k].rearrange("(r b) -> r b", r=32).partition_broadcast(4))
+            parts = vectors[k].rearrange("(r b) -> r b", r=QUAD)
+            queue.dma_start(out=column[k][:], in_=parts.partition_broadcast(P // QUAD))
 
         load_vector(nc.scalar, "gain")
-        nc.scalar.activation(out=warm[:, 1:2], in_=warm[:, 0:1], func=TANH)
         load_x(0, 0, D // 2)
         load_x(0, D // 2, D)
         load_w1(0, 2)
         load_x(1, 0, D)
         load_vector(nc.sync, "bias")
-        load_vector(nc.sync, "rw")
+        load_vector(nc.sync, "weight")
         load_w1(1, 1)
         load_w1(2, 1)
         load_x(2, 0, D)
@@ -93,254 +102,218 @@ def tile_reward_head_terms_h1_kernel(tc, x, w1_words, w1_scales, gain, w2_words,
         for i in range(3, TILES):
             load_x(i, 0, D)
 
-        t = {}
 
-        def live(i):
-            return 0 <= i < TILES
+        tiles = {}
 
-        def x_sort(i, b, on_vector=False):
-            if live(i):
-                x_sorted = once("x_sorted", i, 0, [P, GD, 2, P], F32)
-                words = x_sb[i][:].bitcast(F32).rearrange("m (g p u) -> m g p u", g=GD, u=2)
-                copy = nc.vector.tensor_copy if on_vector else nc.scalar.copy
-                copy(out=x_sorted[:, 2 * b:2 * b + 2].rearrange("m g u p -> m g p u"), in_=words[:, 2 * b:2 * b + 2])
+        def once(kind, i, shape, dtype, c=0):
+            if (kind, i, c) not in tiles:
+                tiles[kind, i, c] = work.tile(shape, dtype, name="%s%d_%d" % (kind, i, c), tag=kind, align_bytes=ALIGN,
+                                              bufs=TANH_BUFS if kind == "tanh_a" else WORK_BUFS)
+            return tiles[kind, i, c]
 
-        def x_turn(i, tags=("x_bank0", "x_bank1")):
-            if not live(i):
-                return
-            if i == 0:
-                words = x_sb[i][:].bitcast(F32).rearrange("m (g p u) -> m g u p", g=GD, u=2)
-            else:
-                words = t["x_sorted", i, 0]
-            groups = GD // len(tags)
-            for b, tag in enumerate(tags):
-                bank = turn.tile([P, groups, 2, P], F32, name="x_bank%d_%d" % (i, b), tag=tag)
-                t["x_bank", i, b] = bank
-                for g in range(groups):
-                    for u in range(2):
-                        nc.tensor.transpose(bank[:, g, u, :], words[:, groups * b + g, u, :], ident[:])
-            t["x_rows", i] = work.tile([P, GD, P, 4], BF16, name="x_rows%d" % i, tag="x_rows", align_bytes=64)
-            t["x_codes", i] = work.tile([P, GD * P], U32, name="x_codes%d" % i, tag="x_codes", align_bytes=64)
-            t["x_scales", i] = work.tile([P, GD * P], U8, name="x_scales%d" % i, tag="x_scales", align_bytes=64)
-
-        def interleave(rows, bank):
-            nc.scalar.copy(out=rows.bitcast(F32), in_=bank.rearrange("p g u r -> p g r u"))
-
-        def quantize(codes, scales, rows):
-            nc.vector.quantize_mx(out=codes.bitcast(FP8X4), scales=scales, in_=rows.rearrange("p g r t -> p (g r t)"))
-
-        def x_copy(i, b, groups=2):
-            if live(i):
-                interleave(t["x_rows", i][:, groups * b:groups * (b + 1)], t["x_bank", i, b][:])
-
-        def x_quant(i, g0, g1):
-            if live(i):
-                quantize(t["x_codes", i][:, g0 * P:g1 * P], t["x_scales", i][:, g0 * P:g1 * P], t["x_rows", i][:, g0:g1])
-
-        def mm1(i, c):
-            if not live(i):
-                return
-            acc = sums.tile([P, GROUP], F32, name="a%d_%d" % (i, c), tag="acc")
-            t["a", i, c] = acc
-            for g in range(GD):
-                nc.tensor.matmul_mx(
-                    out=acc[:],
-                    lhsT=t["x_codes", i][:, g * P:(g + 1) * P].bitcast(FP8X4),
-                    lhsT_scale=t["x_scales", i][:, g * P:(g + 1) * P],
-                    rhs=w1_sb[c][:, g, :].bitcast(FP4X4),
-                    rhs_scale=s1_sb[c][:, g, :],
-                    start=(g == 0), stop=(g == GD - 1))
-
-        def once(kind, i, c, shape, dtype):
-            if (kind, i, c) not in t:
-                t[kind, i, c] = work.tile(shape, dtype, name="%s%d_%d" % (kind, i, c), tag=kind, align_bytes=64,
-                                          bufs=4 if kind == "th" else 3)
-            return t[kind, i, c]
-
-        def by_half(ap, c=0):
-            return ap[:, c * GROUP:(c + 1) * GROUP].rearrange("m (u p e) -> m u p e", u=2, e=2)
-
-        def natural(ap, c=0):
-            return ap[:, c * GROUP:(c + 1) * GROUP].rearrange("m (p u e) -> m u p e", u=2, e=2)
+        def chunk(ap, c):
+            return ap[:, c * GROUP:(c + 1) * GROUP]
 
         def part(size, half):
             return slice(0, size) if half is None else slice(half * size // 2, (half + 1) * size // 2)
 
-        def tanh1(i, c, half=None):
-            if live(i):
-                u = part(2, half)
-                th = once("th", i, c, [P, GROUP], F32)
-                nc.scalar.activation(out=by_half(th)[:, u], in_=natural(t["a", i, c])[:, u], func=TANH)
+        def interleave(rows, bank):
+            nc.scalar.copy(out=rows.bitcast(F32), in_=bank.rearrange("p g u m -> p g m u"))
 
-        def gain_mul(i, c, half=None):
-            if live(i):
-                u = part(2, half)
-                h = once("h", i, 0, [P, F], BF16)
-                nc.vector.tensor_tensor(out=by_half(h, c)[:, u], in0=by_half(t["th", i, c])[:, u],
-                                        in1=by_half(gain_all, c)[:, u], op=MULT)
+        def quantize(codes, scales, rows):
+            nc.vector.quantize_mx(out=codes.bitcast(FP8X4), scales=scales, in_=rows.rearrange("p g m t -> p (g m t)"))
 
-        def h_groups(b):
-            return 2 * b, min(2 * b + 2, GF)
-
-        def h_turn(i, b):
-            if not live(i):
-                return
-            words = t["h", i, 0][:].bitcast(F32)
-            g0, g1 = h_groups(b)
-            bank = turn.tile([P, g1 - g0, 2, P], F32, name="h_bank%d_%d" % (i, b), tag="h_bank%d" % b)
-            t["h_bank", i, b] = bank
-            for g in range(g0, g1):
-                for u in range(2):
-                    w0 = 256 * g + P * u
-                    nc.tensor.transpose(bank[:, g - g0, u, :], words[:, w0:w0 + P], ident[:])
-
-        def h_copy(i, b):
-            if live(i):
-                g0, g1 = h_groups(b)
-                interleave(once("h_rows", i, 0, [P, GF, P, 4], BF16)[:, g0:g1], t["h_bank", i, b][:])
-
-        def h_quant(i, b):
-            if live(i):
-                g0, g1 = h_groups(b)
-                codes = once("h_codes", i, 0, [P, GF * P], U32)
-                scales = once("h_scales", i, 0, [P, GF * P], U8)
-                quantize(codes[:, g0 * P:g1 * P], scales[:, g0 * P:g1 * P], t["h_rows", i, 0][:, g0:g1])
-
-        def mm2(i, c):
-            if not live(i):
-                return
-            acc = sums.tile([P, GROUP], F32, name="z%d_%d" % (i, c), tag="acc")
-            t["z", i, c] = acc
-            for g in range(GF):
-                nc.tensor.matmul_mx(
-                    out=acc[:],
-                    lhsT=t["h_codes", i, 0][:, g * P:(g + 1) * P].bitcast(FP8X4),
-                    lhsT_scale=t["h_scales", i, 0][:, g * P:(g + 1) * P],
-                    rhs=w2_sb[:, g, 2 * c * GROUP:2 * (c + 1) * GROUP].bitcast(FP4X4),
-                    rhs_scale=s2_sb[:, g, c * GROUP:(c + 1) * GROUP],
-                    start=(g == 0), stop=(g == GF - 1))
-
-        def span(c, half):
-            if c is None:
-                return slice(0, N)
-            cols = part(GROUP, half)
-            return slice(c * GROUP + cols.start, c * GROUP + cols.stop)
-
-        def bias_add(i, c, half=None):
-            if live(i):
-                zb = once("zb", i, 0, [P, N], F32)
-                nc.vector.tensor_tensor(out=zb[:, span(c, half)], in0=t["z", i, c][:, part(GROUP, half)],
-                                        in1=bias_all[:, span(c, half)], op=ADD)
-
-        def tanh2(i, c=None, half=None):
-            if live(i):
-                cols = span(c, half)
-                tz = once("tz", i, 0, [P, N], F32)
-                nc.scalar.activation(out=tz[:, cols], in_=t["zb", i, 0][:, cols], func=TANH)
-
-        def weigh(i, c=None, half=None):
-            if live(i):
-                cols = span(c, half)
-                y = once("y", i, 0, [P, N], F32)
-                nc.vector.tensor_tensor(out=y[:, cols], in0=t["tz", i, 0][:, cols], in1=rw_all[:, cols], op=MULT)
-
-        def store_y(i, c=None):
-            if live(i):
-                cols = span(c, None)
-                nc.sync.dma_start(out=out_0[i * P:(i + 1) * P, cols], in_=t["y", i, 0][:, cols])
-
-        def y_round(i, c, half=None, on_scalar=False):
-            if live(i):
-                words = part(P, half)
-                y_bf = once("y_bf", i, 0, [P, N], BF16)
-                copy = nc.scalar.copy if on_scalar else nc.vector.tensor_copy
-                copy(out=by_half(y_bf, c)[:, :, words], in_=natural(t["y", i, 0], c)[:, :, words])
-
-        def y_turn(i, groups=(0, 1), tag="y_bank"):
-            if not live(i):
-                return
-            bank = turn.tile([P, len(groups), 2, P], F32, name="y_bank%d_%d" % (i, groups[0]), tag=tag)
-            t["y_bank", i, groups[0]] = bank
-            for j, g in enumerate(groups):
-                words = t["y_bf", i, 0][:, g * GROUP:(g + 1) * GROUP].bitcast(F32)
-                for u in range(2):
-                    nc.tensor.transpose(bank[:, j, u, :], words[:, P * u:P * (u + 1)], ident[:])
-
-        def y_copy(i, groups=(0, 1)):
-            if live(i):
-                rows = once("y_rows", i, 0, [P, GN, P, 4], BF16)
-                interleave(rows[:, groups[0]:groups[-1] + 1], t["y_bank", i, groups[0]][:])
-
-        codes_hbm = out_1.rearrange("g p m t -> p g (m t)").bitcast(I32)
-
-        def y_quant(i, groups=(0, 1)):
-            if live(i):
-                tok = slice(i * P, (i + 1) * P)
-                for g in groups:
-                    quantize(y_codes[:, g, tok], y_scales[:, g, tok], t["y_rows", i, 0][:, g:g + 1])
-
-        def store_codes(i0, i1, g0=0, g1=GN):
-            span = slice(i0 * P, i1 * P)
-            nc.sync.dma_start(out=codes_hbm[:, g0:g1, span], in_=y_codes[:, g0:g1, span].bitcast(I32))
-
-        def store_pair(i):
-            if i in (1, 3):
-                store_codes(i - 1, i + 1)
-
-        def store_scales(i0, i1, queue):
-            span = slice(i0 * P, i1 * P)
-            for r in range(4):
-                queue.dma_start(
-                    out=out_2[:, r:16:4, span].rearrange("g q m -> q g m").bitcast(I32),
-                    in_=y_scales[r:P:32, :, span].bitcast(I32))
 
         def widen(k):
-            words = column[k][:].bitcast(F32)
-            nc.vector.tensor_copy(out=wide[k][:].rearrange("m (b j) -> m b j", j=32),
-                                  in_=words.unsqueeze(2).to_broadcast([P, words.shape[1], 32]))
+            pairs = column[k][:].bitcast(F32)
+            nc.vector.tensor_copy(out=wide[k][:].rearrange("m (b j) -> m b j", j=QUAD),
+                                  in_=pairs.unsqueeze(2).to_broadcast([P, pairs.shape[1], QUAD]))
 
         def turn_blocks(k):
             nc.vector.transpose(out=turned[k][:], in_=wide[k][:])
 
         def put_in_order(k):
-            nc.scalar.copy(out=spread[k][:].bitcast(F32).rearrange("m (r b) -> m r b", r=32),
-                           in_=turned[k][:].rearrange("m (b r) -> m r b", r=32))
+            nc.scalar.copy(out=spread[k][:].bitcast(F32).rearrange("m (r b) -> m r b", r=QUAD),
+                           in_=turned[k][:].rearrange("m (b r) -> m r b", r=QUAD))
 
         def sort_gain():
-            nc.scalar.copy(out=gain_all[:].bitcast(F32).rearrange("m (c u p) -> m c u p", c=GF, u=2),
-                           in_=spread["gain"][:].bitcast(F32).rearrange("m (c p u) -> m c u p", c=GF, u=2))
+            nc.scalar.copy(out=gain_sorted[:].bitcast(F32).rearrange("m (c u p) -> m c p u", c=GF, u=2),
+                           in_=spread["gain"][:].bitcast(F32).rearrange("m (c p u) -> m c p u", c=GF, u=2))
 
-        def first_layer(i, c):
-            mm1(i, c)
-            tanh1(i, c)
-            gain_mul(i, c)
+
+        def x_sort(i, b, on_vector=False):
+            x_sorted = once("x_sorted", i, [P, GD, 2, P], F32)
+            pairs = x_sb[i][:].bitcast(F32).rearrange("m (g p u) -> m g p u", g=GD, u=2)
+            copy = nc.vector.tensor_copy if on_vector else nc.scalar.copy
+            copy(out=x_sorted[:, 2 * b:2 * b + 2].rearrange("m g u p -> m g p u"), in_=pairs[:, 2 * b:2 * b + 2])
+
+        def x_turn(i, tags=("x_bank0", "x_bank1")):
+            if i == 0:
+                pairs = x_sb[i][:].bitcast(F32).rearrange("m (g p u) -> m g u p", g=GD, u=2)
+            else:
+                pairs = tiles["x_sorted", i, 0]
+            groups = GD // len(tags)
+            for b, tag in enumerate(tags):
+                bank = turn.tile([P, groups, 2, P], F32, name="x_bank%d_%d" % (i, b), tag=tag)
+                tiles["x_bank", i, b] = bank
+                for g in range(groups):
+                    for u in range(2):
+                        nc.tensor.transpose(bank[:, g, u, :], pairs[:, groups * b + g, u, :], ident[:])
+            once("x_rows", i, [P, GD, P, 4], BF16)
+            once("x_codes", i, [P, GD * P], U32)
+            once("x_scales", i, [P, GD * P], U8)
+
+        def x_copy(i, b, groups=2):
+            interleave(tiles["x_rows", i, 0][:, groups * b:groups * (b + 1)], tiles["x_bank", i, b][:])
+
+        def x_quant(i, g0, g1):
+            cols = slice(g0 * P, g1 * P)
+            quantize(tiles["x_codes", i, 0][:, cols], tiles["x_scales", i, 0][:, cols], tiles["x_rows", i, 0][:, g0:g1])
+
+
+        def mm1(i, c):
+            acc = sums.tile([P, GROUP], F32, name="a%d_%d" % (i, c), tag="acc")
+            tiles["a", i, c] = acc
+            for g in range(GD):
+                nc.tensor.matmul_mx(
+                    out=acc[:],
+                    lhsT=tiles["x_codes", i, 0][:, g * P:(g + 1) * P].bitcast(FP8X4),
+                    lhsT_scale=tiles["x_scales", i, 0][:, g * P:(g + 1) * P],
+                    rhs=w1_sb[c][:, g, :].bitcast(FP4X4),
+                    rhs_scale=s1_sb[c][:, g, :],
+                    start=(g == 0), stop=(g == GD - 1))
+
+        def by_u(sorted_chunk):
+            return sorted_chunk.rearrange("m (u p e) -> m u p e", u=2, e=2)
+
+        def tanh1(i, c, half=None):
+            u = part(2, half)
+            tanh_a = once("tanh_a", i, [P, GROUP], F32, c)
+            a = tiles["a", i, c][:].rearrange("m (p u e) -> m u p e", u=2, e=2)
+            nc.scalar.activation(out=by_u(tanh_a[:])[:, u], in_=a[:, u], func=TANH)
+
+        def gain_mul(i, c, half=None):
+            u = part(2, half)
+            h = once("h", i, [P, F], BF16)
+            nc.vector.tensor_tensor(out=by_u(chunk(h, c))[:, u], in0=by_u(tiles["tanh_a", i, c][:])[:, u],
+                                    in1=by_u(chunk(gain_sorted, c))[:, u], op=MULT)
+
+        def h_groups(b):
+            return 2 * b, min(2 * b + 2, GF)
+
+        def h_turn(i, b):
+            pairs = tiles["h", i, 0][:].bitcast(F32)
+            g0, g1 = h_groups(b)
+            bank = turn.tile([P, g1 - g0, 2, P], F32, name="h_bank%d_%d" % (i, b), tag="h_bank%d" % b)
+            tiles["h_bank", i, b] = bank
+            for g in range(g0, g1):
+                for u in range(2):
+                    first = PAIRS * g + P * u
+                    nc.tensor.transpose(bank[:, g - g0, u, :], pairs[:, first:first + P], ident[:])
+
+        def h_copy(i, b):
+            g0, g1 = h_groups(b)
+            interleave(once("h_rows", i, [P, GF, P, 4], BF16)[:, g0:g1], tiles["h_bank", i, b][:])
+
+        def h_quant(i, b):
+            g0, g1 = h_groups(b)
+            codes = once("h_codes", i, [P, GF * P], U32)
+            scales = once("h_scales", i, [P, GF * P], U8)
+            quantize(codes[:, g0 * P:g1 * P], scales[:, g0 * P:g1 * P], tiles["h_rows", i, 0][:, g0:g1])
+
+
+        def mm2(i, c):
+            acc = sums.tile([P, GROUP], F32, name="z%d_%d" % (i, c), tag="acc")
+            tiles["z", i, c] = acc
+            for g in range(GF):
+                nc.tensor.matmul_mx(
+                    out=acc[:],
+                    lhsT=tiles["h_codes", i, 0][:, g * P:(g + 1) * P].bitcast(FP8X4),
+                    lhsT_scale=tiles["h_scales", i, 0][:, g * P:(g + 1) * P],
+                    rhs=w2_sb[:, g, 2 * c * GROUP:2 * (c + 1) * GROUP].bitcast(FP4X4),
+                    rhs_scale=s2_sb[:, g, c * GROUP:(c + 1) * GROUP],
+                    start=(g == 0), stop=(g == GF - 1))
+
+        def bias_add(i, c, half=None):
+            cols = part(GROUP, half)
+            biased = once("biased", i, [P, N], F32)
+            nc.vector.tensor_tensor(out=chunk(biased, c)[:, cols], in0=tiles["z", i, c][:, cols],
+                                    in1=chunk(spread["bias"], c)[:, cols], op=ADD)
+
+        def tanh2(i, c, half=None):
+            cols = part(GROUP, half)
+            tanh_z = once("tanh_z", i, [P, N], F32)
+            nc.scalar.activation(out=chunk(tanh_z, c)[:, cols], in_=chunk(tiles["biased", i, 0], c)[:, cols], func=TANH)
+
+        def weigh(i, c, half=None):
+            cols = part(GROUP, half)
+            y = once("y", i, [P, N], F32)
+            nc.vector.tensor_tensor(out=chunk(y, c)[:, cols], in0=chunk(tiles["tanh_z", i, 0], c)[:, cols],
+                                    in1=chunk(spread["weight"], c)[:, cols], op=MULT)
+
+        def store_y(i, c0=0, c1=GN):
+            cols = slice(c0 * GROUP, c1 * GROUP)
+            nc.sync.dma_start(out=out_0[i * P:(i + 1) * P, cols], in_=tiles["y", i, 0][:, cols])
+
+
+        def y_round(i, c, half=None, on_scalar=False):
+            words = part(P, half)
+            y_sorted = once("y_sorted", i, [P, N], BF16)
+            copy = nc.scalar.copy if on_scalar else nc.vector.tensor_copy
+            copy(out=chunk(y_sorted, c).rearrange("m (u p e) -> m p u e", u=2, e=2)[:, words],
+                 in_=chunk(tiles["y", i, 0], c).rearrange("m (p u e) -> m p u e", u=2, e=2)[:, words])
+
+        def y_turn(i, g0=0, g1=GN, tag="y_bank"):
+            bank = turn.tile([P, g1 - g0, 2, P], F32, name="y_bank%d_%d" % (i, g0), tag=tag)
+            tiles["y_bank", i, g0] = bank
+            for g in range(g0, g1):
+                pairs = chunk(tiles["y_sorted", i, 0], g).bitcast(F32)
+                for u in range(2):
+                    nc.tensor.transpose(bank[:, g - g0, u, :], pairs[:, P * u:P * (u + 1)], ident[:])
+
+        def y_copy(i, g0=0, g1=GN):
+            interleave(once("y_rows", i, [P, GN, P, 4], BF16)[:, g0:g1], tiles["y_bank", i, g0][:])
+
+        def y_quant(i, g0=0, g1=GN):
+            tokens = slice(i * P, (i + 1) * P)
+            for g in range(g0, g1):
+                quantize(y_codes[:, g, tokens], y_scales[:, g, tokens], tiles["y_rows", i, 0][:, g:g + 1])
+
+        codes_hbm = out_1.rearrange("g p m t -> p g (m t)").bitcast(I32)
+
+        def store_codes(i0, i1):
+            tokens = slice(i0 * P, i1 * P)
+            nc.sync.dma_start(out=codes_hbm[:, :, tokens], in_=y_codes[:, :, tokens].bitcast(I32))
+
+        def store_scales(i0, i1, queue):
+            tokens = slice(i0 * P, i1 * P)
+            for r in range(4):
+                queue.dma_start(
+                    out=out_2[:, r:SCALE_ROWS:4, tokens].rearrange("g q m -> q g m").bitcast(I32),
+                    in_=y_scales[r:P:QUAD, :, tokens].bitcast(I32))
 
         x_turn(0, ("x_bank0", "x_bank1", "y_bank", "h_bank0"))
         widen("gain")
         turn_blocks("gain")
-        x_copy(0, 0, 1)
-        x_copy(0, 1, 1)
-        x_copy(0, 2, 1)
-        x_copy(0, 3, 1)
-        x_quant(0, 0, 1)
-        x_quant(0, 1, 2)
-        x_quant(0, 3, 4)
-        x_quant(0, 2, 3)
-        widen("rw")
+        for g in range(GD):
+            x_copy(0, g, 1)
+        for g in (0, 1, 3, 2):
+            x_quant(0, g, g + 1)
+        widen("weight")
         x_sort(1, 0, True)
         x_sort(1, 1, True)
         mm1(0, 0)
         widen("bias")
         put_in_order("gain")
         turn_blocks("bias")
-        sort_gain()
         tanh1(0, 0)
         x_turn(1)
         x_copy(1, 0)
         x_quant(1, 0, 2)
         x_copy(1, 1)
+        sort_gain()
         mm1(0, 1)
-        x_quant(1, 2, 4)
+        x_quant(1, 2, GD)
         mm1(1, 0)
         tanh1(0, 1)
         gain_mul(0, 0)
@@ -349,7 +322,7 @@ def tile_reward_head_terms_h1_kernel(tc, x, w1_words, w1_scales, gain, w2_words,
         gain_mul(0, 1)
         x_sort(2, 0, True)
         tanh1(1, 0)
-        turn_blocks("rw")
+        turn_blocks("weight")
         mm1(1, 1)
         tanh1(0, 2)
         x_sort(2, 1, True)
@@ -373,30 +346,35 @@ def tile_reward_head_terms_h1_kernel(tc, x, w1_words, w1_scales, gain, w2_words,
         x_quant(2, 0, GD)
         bias_add(0, 0)
         tanh1(1, 2)
-        put_in_order("rw")
+        put_in_order("weight")
         mm2(0, 1)
         gain_mul(1, 2)
 
         last = TILES - 1
         for i in range(2, last):
+            has_planes = i >= 3
+            has_sort = i + 2 <= last
             tanh2(i - 2, 0)
             bias_add(i - 2, 1)
             x_turn(i + 1)
             h_turn(i - 1, 0)
             weigh(i - 2, 0)
             h_turn(i - 1, 1)
-            y_turn(i - 3)
+            if has_planes:
+                y_turn(i - 3)
             x_copy(i + 1, 0)
             mm1(i, 0)
             h_copy(i - 1, 1)
             tanh2(i - 2, 1)
-            x_sort(i + 2, 1, True)
+            if has_sort:
+                x_sort(i + 2, 1, True)
             x_copy(i + 1, 1)
             h_copy(i - 1, 0)
             h_quant(i - 1, 1)
             y_round(i - 2, 0)
             mm1(i, 1)
-            y_copy(i - 3)
+            if has_planes:
+                y_copy(i - 3)
             tanh1(i, 0)
             weigh(i - 2, 1)
             x_quant(i + 1, 0, GD)
@@ -407,90 +385,93 @@ def tile_reward_head_terms_h1_kernel(tc, x, w1_words, w1_scales, gain, w2_words,
             store_y(i - 2)
             tanh1(i, 2)
             mm2(i - 1, 0)
-            y_quant(i - 3)
+            if has_planes:
+                y_quant(i - 3)
             gain_mul(i, 0)
             gain_mul(i, 1)
-            x_sort(i + 2, 0)
-            store_pair(i - 3)
+            if has_sort:
+                x_sort(i + 2, 0)
+            if has_planes and i % 2 == 0:
+                store_codes(i - 4, i - 2)
             bias_add(i - 1, 0)
             gain_mul(i, 2)
             mm2(i - 1, 1)
 
-        mm1(7, 0)
-        h_turn(6, 0)
-        bias_add(5, 1)
-        tanh2(5, 0)
-        tanh1(7, 0)
-        y_turn(4)
-        weigh(5, 0)
-        y_round(5, 0)
-        h_turn(6, 1)
-        tanh2(5, 1)
-        h_copy(6, 0)
-        gain_mul(7, 0)
-        weigh(5, 1)
-        h_quant(6, 0)
-        h_copy(6, 1)
-        mm1(7, 1)
-        tanh1(7, 1)
-        y_copy(4)
-        mm1(7, 2)
-        h_quant(6, 1)
-        y_round(5, 1)
-        mm2(6, 0)
-        tanh1(7, 2, 0)
-        tanh1(7, 2, 1)
-        gain_mul(7, 1)
-        store_y(5)
-        gain_mul(7, 2, 0)
-        h_turn(7, 0)
-        h_copy(7, 0)
-        gain_mul(7, 2, 1)
-        bias_add(6, 0)
-        y_turn(5)
-        h_quant(7, 0)
-        h_turn(7, 1)
-        y_quant(4)
-        h_copy(7, 1)
-        mm2(6, 1)
-        tanh2(6, 0)
-        h_quant(7, 1)
-        mm2(7, 0)
-        y_copy(5)
-        bias_add(6, 1)
-        mm2(7, 1)
-        weigh(6, 0)
-        bias_add(7, 0)
-        tanh2(6, 1)
-        bias_add(7, 1, 0)
-        y_round(6, 0, None, True)
-        tanh2(7, 0)
-        bias_add(7, 1, 1)
-        weigh(6, 1)
-        tanh2(7, 1, 0)
-        weigh(7, 0)
-        weigh(7, 1, 0)
-        store_codes(4, 5)
-        tanh2(7, 1, 1)
-        y_round(6, 1, None, True)
-        y_turn(6)
-        weigh(7, 1, 1)
-        y_copy(6)
-        y_round(7, 0)
-        y_turn(7, (0,), "x_bank0")
-        store_scales(0, 5, nc.sync)
-        store_y(6)
-        y_copy(7, (0,))
-        y_round(7, 1, 0)
-        y_round(7, 1, 1)
-        y_quant(5)
-        store_y(7, 0)
-        y_quant(6)
-        y_turn(7, (1,), "x_bank1")
-        y_copy(7, (1,))
-        store_y(7, 1)
-        store_codes(5, 7)
-        y_quant(7, (0,))
-        y_quant(7, (1,))
-        store_codes(7, 8)
-        store_scales(5, 8, nc.scalar)
+        mm1(last, 0)
+        h_turn(last - 1, 0)
+        bias_add(last - 2, 1)
+        tanh2(last - 2, 0)
+        tanh1(last, 0)
+        y_turn(last - 3)
+        weigh(last - 2, 0)
+        y_round(last - 2, 0)
+        h_turn(last - 1, 1)
+        tanh2(last - 2, 1)
+        h_copy(last - 1, 0)
+        gain_mul(last, 0)
+        weigh(last - 2, 1)
+        h_quant(last - 1, 0)
+        h_copy(last - 1, 1)
+        mm1(last, 1)
+        tanh1(last, 1)
+        y_copy(last - 3)
+        mm1(last, 2)
+        h_quant(last - 1, 1)
+        y_round(last - 2, 1)
+        mm2(last - 1, 0)
+        tanh1(last, 2, 0)
+        tanh1(last, 2, 1)
+        gain_mul(last, 1)
+        store_y(last - 2)
+        gain_mul(last, 2, 0)
+        h_turn(last, 0)
+        h_copy(last, 0)
+        gain_mul(last, 2, 1)
+        bias_add(last - 1, 0)
+        y_turn(last - 2)
+        h_quant(last, 0)
+        h_turn(last, 1)
+        y_quant(last - 3)
+        h_copy(last, 1)
+        mm2(last - 1, 1)
+        tanh2(last - 1, 0)
+        h_quant(last, 1)
+        mm2(last, 0)
+        y_copy(last - 2)
+        bias_add(last - 1, 1)
+        mm2(last, 1)
+        weigh(last - 1, 0)
+        bias_add(last, 0)
+        tanh2(last - 1, 1)
+        bias_add(last, 1, 0)
+        y_round(last - 1, 0, on_scalar=True)
+        tanh2(last, 0)
+        bias_add(last, 1, 1)
+        weigh(last - 1, 1)
+        tanh2(last, 1, 0)
+        weigh(last, 0)
+        weigh(last, 1, 0)
+        store_codes(last - 3, last - 2)
+        tanh2(last, 1, 1)
+        y_round(last - 1, 1, on_scalar=True)
+        y_turn(last - 1)
+        weigh(last, 1, 1)
+        y_copy(last - 1)
+        y_round(last, 0)
+        y_turn(last, 0, 1, "x_bank0")
+        store_scales(0, last - 2, nc.sync)
+        store_y(last - 1)
+        y_copy(last, 0, 1)
+        y_round(last, 1, 0)
+        y_round(last, 1, 1)
+        y_quant(last - 2)
+        store_y(last, 0, 1)
+        y_quant(last - 1)
+        y_turn(last, 1, 2, "x_bank1")
+        y_copy(last, 1, 2)
+        store_y(last, 1, 2)
+        store_codes(last - 2, last)
+        y_quant(last, 0, 1)
+        y_quant(last, 1, 2)
+        store_codes(last, TILES)
+        store_scales(last - 2, TILES, nc.scalar)

from contextlib import ExitStack

import concourse.mybir as mybir
from concourse.masks import make_identity

M, D, F, N = 1024, 2048, 1536, 1024
FLOPS = 2 * M * (D * F + F * N)

F32 = mybir.dt.float32
BF16 = mybir.dt.bfloat16
I32 = mybir.dt.int32
U32 = mybir.dt.uint32
U8 = mybir.dt.uint8
FP8X4 = mybir.dt.float8_e4m3fn_x4
FP4X4 = mybir.dt.float4_e2m1fn_x4
TANH = mybir.ActivationFunctionType.Tanh
ADD = mybir.AluOpType.add
MULT = mybir.AluOpType.mult

P = 128
QUAD = 32
GROUP = 512
PAIRS = GROUP // 2
SCALE_ROWS = GROUP // 32
TILES = M // P
GD, GF, GN = D // GROUP, F // GROUP, N // GROUP
ALIGN = 64
WORK_BUFS = 3
TANH_BUFS = 4
SUM_BANKS = 3


def tile_reward_head_terms_h1_kernel(tc, x, w1_words, w1_scales, gain, w2_words, w2_scales, bias,
                                                reward_weight, out_0, out_1, out_2):
    nc = tc.nc
    with ExitStack() as ctx:
        keep = ctx.enter_context(tc.tile_pool(name="keep", bufs=1))
        work = ctx.enter_context(tc.tile_pool(name="work", bufs=WORK_BUFS))
        turn = ctx.enter_context(tc.psum_pool(name="turn", bufs=1))
        sums = ctx.enter_context(tc.psum_pool(name="sums", bufs=SUM_BANKS))
        ctx.enter_context(tc.manual_schedule())

        ident = keep.tile([P, P], F32, name="ident", align_bytes=ALIGN)
        make_identity(nc, ident[:])

        x_sb = [keep.tile([P, D], BF16, name="x_sb%d" % i, align_bytes=ALIGN) for i in range(TILES)]
        w1_sb = [keep.tile([P, GD, 2 * GROUP], U8, name="w1_sb%d" % c, align_bytes=ALIGN) for c in range(GF)]
        s1_sb = [keep.tile([P, GD, GROUP], U8, name="s1_sb%d" % c, align_bytes=ALIGN) for c in range(GF)]
        w2_sb = keep.tile([P, GF, 2 * N], U8, name="w2_sb", align_bytes=ALIGN)
        s2_sb = keep.tile([P, GF, N], U8, name="s2_sb", align_bytes=ALIGN)
        gain_sorted = keep.tile([P, F], BF16, name="gain_sorted", align_bytes=ALIGN)
        vectors = {"gain": gain, "bias": bias, "weight": reward_weight}
        column = {k: keep.tile([P, v.shape[0] // QUAD], BF16, name=k + "_column", align_bytes=ALIGN)
                  for k, v in vectors.items()}
        wide = {k: keep.tile([P, v.shape[0] // 2], F32, name=k + "_wide", align_bytes=ALIGN)
                for k, v in vectors.items()}
        turned = {k: keep.tile([P, v.shape[0] // 2], F32, name=k + "_turned", align_bytes=ALIGN)
                  for k, v in vectors.items()}
        spread = {k: keep.tile([P, v.shape[0]], BF16, name=k + "_spread", align_bytes=ALIGN)
                  for k, v in vectors.items()}
        y_codes = keep.tile([P, GN, M], U32, name="y_codes", align_bytes=ALIGN)
        y_scales = keep.tile([P, GN, M], U8, name="y_scales", align_bytes=ALIGN)

        for c in range(GF):
            nc.vector.memset(s1_sb[c][:].rearrange("p g n -> p (g n)").bitcast(I32), 0)
        nc.vector.memset(s2_sb[:].rearrange("p g n -> p (g n)").bitcast(I32), 0)


        def load_x(i, k0, k1):
            nc.sync.dma_start(out=x_sb[i][:, k0:k1], in_=x[i * P:(i + 1) * P, k0:k1])

        def load_scales(plane, rows, n0, n1):
            for r in range(4):
                nc.sync.dma_start(
                    out=plane[r:P:QUAD].bitcast(I32),
                    in_=rows[:, r:SCALE_ROWS:4, n0:n1].rearrange("g q n -> q g n").bitcast(I32))

        def load_w1(c, pieces):
            load_scales(s1_sb[c], w1_scales, c * GROUP, (c + 1) * GROUP)
            step = GD // pieces
            for g in range(0, GD, step):
                words = w1_words[g:g + step, :, 2 * c * GROUP:2 * (c + 1) * GROUP]
                nc.sync.dma_start(out=w1_sb[c][:, g:g + step, :].bitcast(I32),
                                  in_=words.rearrange("g p b -> p g b").bitcast(I32))

        def load_vector(queue, k):
            parts = vectors[k].rearrange("(r b) -> r b", r=QUAD)
            queue.dma_start(out=column[k][:], in_=parts.partition_broadcast(P // QUAD))

        load_vector(nc.scalar, "gain")
        load_x(0, 0, D // 2)
        load_x(0, D // 2, D)
        load_w1(0, 2)
        load_x(1, 0, D)
        load_vector(nc.sync, "bias")
        load_vector(nc.sync, "weight")
        load_w1(1, 1)
        load_w1(2, 1)
        load_x(2, 0, D)
        load_scales(s2_sb, w2_scales, 0, N)
        nc.sync.dma_start(out=w2_sb[:].bitcast(I32), in_=w2_words.rearrange("g p b -> p g b").bitcast(I32))
        for i in range(3, TILES):
            load_x(i, 0, D)


        tiles = {}

        def once(kind, i, shape, dtype, c=0):
            if (kind, i, c) not in tiles:
                tiles[kind, i, c] = work.tile(shape, dtype, name="%s%d_%d" % (kind, i, c), tag=kind, align_bytes=ALIGN,
                                              bufs=TANH_BUFS if kind == "tanh_a" else WORK_BUFS)
            return tiles[kind, i, c]

        def chunk(ap, c):
            return ap[:, c * GROUP:(c + 1) * GROUP]

        def part(size, half):
            return slice(0, size) if half is None else slice(half * size // 2, (half + 1) * size // 2)

        def interleave(rows, bank):
            nc.scalar.copy(out=rows.bitcast(F32), in_=bank.rearrange("p g u m -> p g m u"))

        def quantize(codes, scales, rows):
            nc.vector.quantize_mx(out=codes.bitcast(FP8X4), scales=scales, in_=rows.rearrange("p g m t -> p (g m t)"))


        def widen(k):
            pairs = column[k][:].bitcast(F32)
            nc.vector.tensor_copy(out=wide[k][:].rearrange("m (b j) -> m b j", j=QUAD),
                                  in_=pairs.unsqueeze(2).to_broadcast([P, pairs.shape[1], QUAD]))

        def turn_blocks(k):
            nc.vector.transpose(out=turned[k][:], in_=wide[k][:])

        def put_in_order(k):
            nc.scalar.copy(out=spread[k][:].bitcast(F32).rearrange("m (r b) -> m r b", r=QUAD),
                           in_=turned[k][:].rearrange("m (b r) -> m r b", r=QUAD))

        def sort_gain():
            nc.scalar.copy(out=gain_sorted[:].bitcast(F32).rearrange("m (c u p) -> m c p u", c=GF, u=2),
                           in_=spread["gain"][:].bitcast(F32).rearrange("m (c p u) -> m c p u", c=GF, u=2))


        def x_sort(i, b, on_vector=False):
            x_sorted = once("x_sorted", i, [P, GD, 2, P], F32)
            pairs = x_sb[i][:].bitcast(F32).rearrange("m (g p u) -> m g p u", g=GD, u=2)
            copy = nc.vector.tensor_copy if on_vector else nc.scalar.copy
            copy(out=x_sorted[:, 2 * b:2 * b + 2].rearrange("m g u p -> m g p u"), in_=pairs[:, 2 * b:2 * b + 2])

        def x_turn(i, tags=("x_bank0", "x_bank1")):
            if i == 0:
                pairs = x_sb[i][:].bitcast(F32).rearrange("m (g p u) -> m g u p", g=GD, u=2)
            else:
                pairs = tiles["x_sorted", i, 0]
            groups = GD // len(tags)
            for b, tag in enumerate(tags):
                bank = turn.tile([P, groups, 2, P], F32, name="x_bank%d_%d" % (i, b), tag=tag)
                tiles["x_bank", i, b] = bank
                for g in range(groups):
                    for u in range(2):
                        nc.tensor.transpose(bank[:, g, u, :], pairs[:, groups * b + g, u, :], ident[:])
            once("x_rows", i, [P, GD, P, 4], BF16)
            once("x_codes", i, [P, GD * P], U32)
            once("x_scales", i, [P, GD * P], U8)

        def x_copy(i, b, groups=2):
            interleave(tiles["x_rows", i, 0][:, groups * b:groups * (b + 1)], tiles["x_bank", i, b][:])

        def x_quant(i, g0, g1):
            cols = slice(g0 * P, g1 * P)
            quantize(tiles["x_codes", i, 0][:, cols], tiles["x_scales", i, 0][:, cols], tiles["x_rows", i, 0][:, g0:g1])


        def mm1(i, c):
            acc = sums.tile([P, GROUP], F32, name="a%d_%d" % (i, c), tag="acc")
            tiles["a", i, c] = acc
            for g in range(GD):
                nc.tensor.matmul_mx(
                    out=acc[:],
                    lhsT=tiles["x_codes", i, 0][:, g * P:(g + 1) * P].bitcast(FP8X4),
                    lhsT_scale=tiles["x_scales", i, 0][:, g * P:(g + 1) * P],
                    rhs=w1_sb[c][:, g, :].bitcast(FP4X4),
                    rhs_scale=s1_sb[c][:, g, :],
                    start=(g == 0), stop=(g == GD - 1))

        def by_u(sorted_chunk):
            return sorted_chunk.rearrange("m (u p e) -> m u p e", u=2, e=2)

        def tanh1(i, c, half=None):
            u = part(2, half)
            tanh_a = once("tanh_a", i, [P, GROUP], F32, c)
            a = tiles["a", i, c][:].rearrange("m (p u e) -> m u p e", u=2, e=2)
            nc.scalar.activation(out=by_u(tanh_a[:])[:, u], in_=a[:, u], func=TANH)

        def gain_mul(i, c, half=None):
            u = part(2, half)
            h = once("h", i, [P, F], BF16)
            nc.vector.tensor_tensor(out=by_u(chunk(h, c))[:, u], in0=by_u(tiles["tanh_a", i, c][:])[:, u],
                                    in1=by_u(chunk(gain_sorted, c))[:, u], op=MULT)

        def h_groups(b):
            return 2 * b, min(2 * b + 2, GF)

        def h_turn(i, b):
            pairs = tiles["h", i, 0][:].bitcast(F32)
            g0, g1 = h_groups(b)
            bank = turn.tile([P, g1 - g0, 2, P], F32, name="h_bank%d_%d" % (i, b), tag="h_bank%d" % b)
            tiles["h_bank", i, b] = bank
            for g in range(g0, g1):
                for u in range(2):
                    first = PAIRS * g + P * u
                    nc.tensor.transpose(bank[:, g - g0, u, :], pairs[:, first:first + P], ident[:])

        def h_copy(i, b):
            g0, g1 = h_groups(b)
            interleave(once("h_rows", i, [P, GF, P, 4], BF16)[:, g0:g1], tiles["h_bank", i, b][:])

        def h_quant(i, b):
            g0, g1 = h_groups(b)
            codes = once("h_codes", i, [P, GF * P], U32)
            scales = once("h_scales", i, [P, GF * P], U8)
            quantize(codes[:, g0 * P:g1 * P], scales[:, g0 * P:g1 * P], tiles["h_rows", i, 0][:, g0:g1])


        def mm2(i, c):
            acc = sums.tile([P, GROUP], F32, name="z%d_%d" % (i, c), tag="acc")
            tiles["z", i, c] = acc
            for g in range(GF):
                nc.tensor.matmul_mx(
                    out=acc[:],
                    lhsT=tiles["h_codes", i, 0][:, g * P:(g + 1) * P].bitcast(FP8X4),
                    lhsT_scale=tiles["h_scales", i, 0][:, g * P:(g + 1) * P],
                    rhs=w2_sb[:, g, 2 * c * GROUP:2 * (c + 1) * GROUP].bitcast(FP4X4),
                    rhs_scale=s2_sb[:, g, c * GROUP:(c + 1) * GROUP],
                    start=(g == 0), stop=(g == GF - 1))

        def bias_add(i, c, half=None):
            cols = part(GROUP, half)
            biased = once("biased", i, [P, N], F32)
            nc.vector.tensor_tensor(out=chunk(biased, c)[:, cols], in0=tiles["z", i, c][:, cols],
                                    in1=chunk(spread["bias"], c)[:, cols], op=ADD)

        def tanh2(i, c, half=None):
            cols = part(GROUP, half)
            tanh_z = once("tanh_z", i, [P, N], F32)
            nc.scalar.activation(out=chunk(tanh_z, c)[:, cols], in_=chunk(tiles["biased", i, 0], c)[:, cols], func=TANH)

        def weigh(i, c, half=None):
            cols = part(GROUP, half)
            y = once("y", i, [P, N], F32)
            nc.vector.tensor_tensor(out=chunk(y, c)[:, cols], in0=chunk(tiles["tanh_z", i, 0], c)[:, cols],
                                    in1=chunk(spread["weight"], c)[:, cols], op=MULT)

        def store_y(i, c0=0, c1=GN):
            cols = slice(c0 * GROUP, c1 * GROUP)
            nc.sync.dma_start(out=out_0[i * P:(i + 1) * P, cols], in_=tiles["y", i, 0][:, cols])


        def y_round(i, c, half=None, on_scalar=False):
            words = part(P, half)
            y_sorted = once("y_sorted", i, [P, N], BF16)
            copy = nc.scalar.copy if on_scalar else nc.vector.tensor_copy
            copy(out=chunk(y_sorted, c).rearrange("m (u p e) -> m p u e", u=2, e=2)[:, words],
                 in_=chunk(tiles["y", i, 0], c).rearrange("m (p u e) -> m p u e", u=2, e=2)[:, words])

        def y_turn(i, g0=0, g1=GN, tag="y_bank"):
            bank = turn.tile([P, g1 - g0, 2, P], F32, name="y_bank%d_%d" % (i, g0), tag=tag)
            tiles["y_bank", i, g0] = bank
            for g in range(g0, g1):
                pairs = chunk(tiles["y_sorted", i, 0], g).bitcast(F32)
                for u in range(2):
                    nc.tensor.transpose(bank[:, g - g0, u, :], pairs[:, P * u:P * (u + 1)], ident[:])

        def y_copy(i, g0=0, g1=GN):
            interleave(once("y_rows", i, [P, GN, P, 4], BF16)[:, g0:g1], tiles["y_bank", i, g0][:])

        def y_quant(i, g0=0, g1=GN):
            tokens = slice(i * P, (i + 1) * P)
            for g in range(g0, g1):
                quantize(y_codes[:, g, tokens], y_scales[:, g, tokens], tiles["y_rows", i, 0][:, g:g + 1])

        codes_hbm = out_1.rearrange("g p m t -> p g (m t)").bitcast(I32)

        def store_codes(i0, i1):
            tokens = slice(i0 * P, i1 * P)
            nc.sync.dma_start(out=codes_hbm[:, :, tokens], in_=y_codes[:, :, tokens].bitcast(I32))

        def store_scales(i0, i1, queue):
            tokens = slice(i0 * P, i1 * P)
            for r in range(4):
                queue.dma_start(
                    out=out_2[:, r:SCALE_ROWS:4, tokens].rearrange("g q m -> q g m").bitcast(I32),
                    in_=y_scales[r:P:QUAD, :, tokens].bitcast(I32))

        x_turn(0, ("x_bank0", "x_bank1", "y_bank", "h_bank0"))
        widen("gain")
        turn_blocks("gain")
        for g in range(GD):
            x_copy(0, g, 1)
        for g in (0, 1, 3, 2):
            x_quant(0, g, g + 1)
        widen("weight")
        x_sort(1, 0, True)
        x_sort(1, 1, True)
        mm1(0, 0)
        widen("bias")
        put_in_order("gain")
        turn_blocks("bias")
        tanh1(0, 0)
        x_turn(1)
        x_copy(1, 0)
        x_quant(1, 0, 2)
        x_copy(1, 1)
        sort_gain()
        mm1(0, 1)
        x_quant(1, 2, GD)
        mm1(1, 0)
        tanh1(0, 1)
        gain_mul(0, 0)
        put_in_order("bias")
        mm1(0, 2)
        gain_mul(0, 1)
        x_sort(2, 0, True)
        tanh1(1, 0)
        turn_blocks("weight")
        mm1(1, 1)
        tanh1(0, 2)
        x_sort(2, 1, True)
        tanh1(1, 1)
        h_turn(0, 0)
        x_turn(2)
        gain_mul(0, 2)
        h_copy(0, 0)
        h_turn(0, 1)
        x_copy(2, 1)
        h_copy(0, 1)
        x_copy(2, 0)
        mm1(1, 2)
        gain_mul(1, 0)
        h_quant(0, 0)
        gain_mul(1, 1)
        h_quant(0, 1)
        mm2(0, 0)
        x_sort(3, 1, True)
        x_sort(3, 0)
        x_quant(2, 0, GD)
        bias_add(0, 0)
        tanh1(1, 2)
        put_in_order("weight")
        mm2(0, 1)
        gain_mul(1, 2)

        last = TILES - 1
        for i in range(2, last):
            has_planes = i >= 3
            has_sort = i + 2 <= last
            tanh2(i - 2, 0)
            bias_add(i - 2, 1)
            x_turn(i + 1)
            h_turn(i - 1, 0)
            weigh(i - 2, 0)
            h_turn(i - 1, 1)
            if has_planes:
                y_turn(i - 3)
            x_copy(i + 1, 0)
            mm1(i, 0)
            h_copy(i - 1, 1)
            tanh2(i - 2, 1)
            if has_sort:
                x_sort(i + 2, 1, True)
            x_copy(i + 1, 1)
            h_copy(i - 1, 0)
            h_quant(i - 1, 1)
            y_round(i - 2, 0)
            mm1(i, 1)
            if has_planes:
                y_copy(i - 3)
            tanh1(i, 0)
            weigh(i - 2, 1)
            x_quant(i + 1, 0, GD)
            h_quant(i - 1, 0)
            mm1(i, 2)
            y_round(i - 2, 1)
            tanh1(i, 1)
            store_y(i - 2)
            tanh1(i, 2)
            mm2(i - 1, 0)
            if has_planes:
                y_quant(i - 3)
            gain_mul(i, 0)
            gain_mul(i, 1)
            if has_sort:
                x_sort(i + 2, 0)
            if has_planes and i % 2 == 0:
                store_codes(i - 4, i - 2)
            bias_add(i - 1, 0)
            gain_mul(i, 2)
            mm2(i - 1, 1)

        mm1(last, 0)
        h_turn(last - 1, 0)
        bias_add(last - 2, 1)
        tanh2(last - 2, 0)
        tanh1(last, 0)
        y_turn(last - 3)
        weigh(last - 2, 0)
        y_round(last - 2, 0)
        h_turn(last - 1, 1)
        tanh2(last - 2, 1)
        h_copy(last - 1, 0)
        gain_mul(last, 0)
        weigh(last - 2, 1)
        h_quant(last - 1, 0)
        h_copy(last - 1, 1)
        mm1(last, 1)
        tanh1(last, 1)
        y_copy(last - 3)
        mm1(last, 2)
        h_quant(last - 1, 1)
        y_round(last - 2, 1)
        mm2(last - 1, 0)
        tanh1(last, 2, 0)
        tanh1(last, 2, 1)
        gain_mul(last, 1)
        store_y(last - 2)
        gain_mul(last, 2, 0)
        h_turn(last, 0)
        h_copy(last, 0)
        gain_mul(last, 2, 1)
        bias_add(last - 1, 0)
        y_turn(last - 2)
        h_quant(last, 0)
        h_turn(last, 1)
        y_quant(last - 3)
        h_copy(last, 1)
        mm2(last - 1, 1)
        tanh2(last - 1, 0)
        h_quant(last, 1)
        mm2(last, 0)
        y_copy(last - 2)
        bias_add(last - 1, 1)
        mm2(last, 1)
        weigh(last - 1, 0)
        bias_add(last, 0)
        tanh2(last - 1, 1)
        bias_add(last, 1, 0)
        y_round(last - 1, 0, on_scalar=True)
        tanh2(last, 0)
        bias_add(last, 1, 1)
        weigh(last - 1, 1)
        tanh2(last, 1, 0)
        weigh(last, 0)
        weigh(last, 1, 0)
        store_codes(last - 3, last - 2)
        tanh2(last, 1, 1)
        y_round(last - 1, 1, on_scalar=True)
        y_turn(last - 1)
        weigh(last, 1, 1)
        y_copy(last - 1)
        y_round(last, 0)
        y_turn(last, 0, 1, "x_bank0")
        store_scales(0, last - 2, nc.sync)
        store_y(last - 1)
        y_copy(last, 0, 1)
        y_round(last, 1, 0)
        y_round(last, 1, 1)
        y_quant(last - 2)
        store_y(last, 0, 1)
        y_quant(last - 1)
        y_turn(last, 1, 2, "x_bank1")
        y_copy(last, 1, 2)
        store_y(last, 1, 2)
        store_codes(last - 2, last)
        y_quant(last, 0, 1)
        y_quant(last, 1, 2)
        store_codes(last, TILES)
        store_scales(last - 2, TILES, nc.scalar)
